import numpy as np
import ml_dtypes


def mxq(x, axis, fmt="e4m3"):
    dtype, down = {"e4m3": (ml_dtypes.float8_e4m3fn, 7), "e5m2": (ml_dtypes.float8_e5m2, 14)}[fmt]
    v = np.moveaxis(np.asarray(x, np.float32).astype(ml_dtypes.bfloat16).astype(np.float64), axis, -1)
    blocks = v.reshape(v.shape[:-1] + (-1, 32))
    amax = np.abs(blocks).max(-1, keepdims=True)
    byte = np.maximum(np.where(amax > 0, np.frexp(amax)[1] - 1 + 127, 0) - down, 1)
    scale = np.exp2(byte - 127.0)
    codes = (blocks / scale).astype(np.float32).astype(dtype).astype(np.float64)
    return np.moveaxis((codes * scale).reshape(v.shape), -1, axis)


WIDE = False


def mx_kscale(k):
    if not WIDE:
        return np.ones(k)
    levels = np.array([10, -10, 5, -5, 0])
    if k % 512:
        return np.exp2(np.random.permutation(np.resize(levels, k // 32))).repeat(32)
    a = np.empty((k // 512, 16))
    for p in range(k // 512):
        a[p, :8] = np.random.permutation(np.resize(levels, 8))
        for g in range(8):
            far = levels[np.abs(levels - a[p, g]) >= 10]
            a[p, g + 8] = far[np.random.randint(len(far))]
    return np.exp2(a.ravel()).repeat(32)


def f64(x):
    return np.asarray(x).astype(np.float64)


def striped(idx):
    return np.tile(idx.reshape(-1, 16).T, (8, 1)).astype(np.uint16)


def unstriped(offs):
    return offs[:16].T.reshape(-1).astype(np.int64)


def pack_weight(w):
    k, n = w.shape
    w = f64(np.asarray(w, np.float32).astype(ml_dtypes.bfloat16)).reshape(k // 32, 32, n)
    amax = np.abs(w).max(1)
    byte = np.clip(np.where(amax > 0, np.frexp(amax)[1] - 1 + 127 - 7, 1), 1, 254)
    scaled = (w * np.exp2(127.0 - byte)[:, None, :]).reshape(k, n).astype(np.float32)
    words = np.ascontiguousarray(scaled.reshape(k // 512, 128, 4, n).transpose(0, 1, 3, 2)).astype(ml_dtypes.float8_e4m3fn).view(np.uint8)
    return words, np.ascontiguousarray(byte.astype(np.uint8).reshape(k // 512, 16, n))


def unpack_weight(words, scales):
    g, p, n, _ = words.shape
    vals = np.ascontiguousarray(words).view(ml_dtypes.float8_e4m3fn).astype(np.float64) * np.repeat(np.exp2(scales.astype(np.float64) - 127.0), 8, axis=1)[..., None]
    return vals.transpose(0, 1, 3, 2).reshape(g * 512, n)


def gelu(v):
    return 0.5 * v * (1.0 + np.tanh(np.sqrt(2.0 / np.pi) * (v + 0.044715 * v**3)))


K, T, S, N = 1024, 1024, 512, 256
P = 2 ** 7


def setup_inputs():
    n = np.random.standard_normal
    s = mx_kscale(K)[:, None]
    packed_w1 = pack_weight(n((K, N)) / np.sqrt(K) / s)
    return {
        "xT": (n((K, T)) * s).astype(np.float32),
        "zp": np.tile(np.random.uniform(-0.6, 0.6, T), (P, 1)).astype(np.float32),
        "csum": n((N, 1)).astype(np.float32),
        "w1_words": packed_w1[0],
        "w1_scales": packed_w1[1],
        "offs": striped(np.random.permutation(T)[:S]),
    }


def reference(xT, zp, csum, w1_words, w1_scales, offs):
    xq = mxq(f64(xT)[:, unstriped(offs)], 0, "e4m3")
    y = unpack_weight(w1_words, w1_scales).T @ xq
    zg = f64(zp)[:1][:, unstriped(offs)]
    return gelu(y - (f64(csum) * zg))

@@ -1,0 +1,159 @@
+from contextlib import ExitStack
+
+import concourse.mybir as mybir
+from concourse.masks import make_identity
+
+K, T, S, N = 1024, 1024, 512, 256
+FLOPS = 2 * K * S * N
+
+F32 = mybir.dt.float32
+BF16 = mybir.dt.bfloat16
+I32 = mybir.dt.int32
+U32 = mybir.dt.uint32
+U16 = mybir.dt.uint16
+U8 = mybir.dt.uint8
+FP8X4 = mybir.dt.float8_e4m3fn_x4
+GELU = mybir.ActivationFunctionType.Gelu_apprx_tanh
+MULT = mybir.AluOpType.mult
+SUBTRACT = mybir.AluOpType.subtract
+
+P = 128
+K_PASS = 512
+PASSES = K // K_PASS
+HALVES = N // P
+T_HALF = T // 2
+CHUNK = 128
+CHUNKS = S // CHUNK
+SCALAR_SHARE = 176
+ZP_RUN = T // P
+
+
+def tile_picked_zeropt_gelu_l_kernel(tc, xT, zp, csum, w1_words, w1_scales, offs, out):
+    nc = tc.nc
+    with ExitStack() as ctx:
+        keep = ctx.enter_context(tc.tile_pool(name="keep", bufs=1))
+        psum = ctx.enter_context(tc.psum_pool(name="psum", bufs=1))
+
+        offsets = keep.tile([P, S // 16], U16, name="offsets")
+        zp_runs = keep.tile([P, ZP_RUN], F32, name="zp_runs")
+        nc.scalar.dma_start(zp_runs[:], zp[0, :].rearrange("(p r) -> p r", r=ZP_RUN))
+
+        raw = {}
+        for z in range(PASSES):
+            rows = xT[z * K_PASS : (z + 1) * K_PASS, :].rearrange("(p u e) t -> p u e t", u=2, e=2)
+            for u in range(2):
+                for h in range(2):
+                    raw[z, u, h] = keep.tile([P, 2, T_HALF], F32, name=f"raw{z}{u}{h}")
+                    nc.sync.dma_start(raw[z, u, h][:], rows[:, u, :, h * T_HALF : (h + 1) * T_HALF])
+                    if (z, u, h) == (0, 0, 0):
+                        nc.sync.dma_start(offsets[:], offs)
+
+        w_scales = keep.tile([P, PASSES, N], U8, name="w_scales", align_bytes=64)
+        nc.gpsimd.memset(w_scales[:].rearrange("p z n -> p (z n)").bitcast(I32), 0)
+        w_codes = []
+        for z in range(PASSES):
+            w_codes.append(keep.tile([P, N], U32, name=f"w_codes{z}", align_bytes=64))
+            nc.sync.dma_start(w_codes[z][:].bitcast(I32), w1_words[z].rearrange("p n t -> p (n t)").bitcast(I32))
+        for q in range(4):
+            nc.sync.dma_start(
+                w_scales[32 * q : 32 * q + 4, :, :].bitcast(I32),
+                w1_scales[:, 4 * q : 4 * q + 4, :].rearrange("z r n -> r z n").bitcast(I32),
+            )
+        csum_cols = keep.tile([P, HALVES], F32, name="csum_cols")
+        with nc.allow_non_contiguous_dma(reason="one value to a partition"):
+            nc.sync.dma_start(csum_cols[:], csum.rearrange("(h p) o -> p (h o)", p=P))
+
+        zero_in = keep.tile([P, 1], F32, name="zero_in")
+        zero_bias = keep.tile([P, 1], F32, name="zero_bias")
+        nc.vector.memset(zero_in[:], 0.0)
+        nc.scalar.activation(zero_bias[:], zero_in[:], GELU)
+
+        identity = keep.tile([P, P], F32, name="identity")
+        make_identity(nc, identity[:])
+        zp_table = keep.tile([P, T], F32, name="zp_table")
+        zp_by_run = zp_table[:].rearrange("p (n r) -> p n r", r=ZP_RUN)
+        for b in range(2):
+            spread = psum.tile([P, 4, P], F32, name="spread", tag=f"bank{b}")
+            for r in range(4):
+                column = zp_runs[:, 4 * b + r : 4 * b + r + 1].to_broadcast([P, P])
+                nc.tensor.transpose(spread[:, r, :], column, identity[:])
+            nc.vector.tensor_copy(zp_by_run[:, :, 4 * b : 4 * b + 4], spread[:].rearrange("p r n -> p n r"))
+        zp_picked = keep.tile([P, S], F32, name="zp_picked")
+        nc.vector.tensor_copy(zp_picked[:], zp_table[:].indirect(offsets[:]))
+
+        def cast_pair(z, u):
+            pairs = keep.tile([P, 2 * T], BF16, name=f"pairs{z}{u}")
+            view = pairs[:].rearrange("p (t e) -> p t e", e=2)
+            first, second = (raw[z, u, h][:].rearrange("p e t -> p t e") for h in range(2))
+            nc.scalar.copy(view[:, :T_HALF, :], first)
+            nc.scalar.copy(view[:, T_HALF : T_HALF + SCALAR_SHARE, :], second[:, :SCALAR_SHARE, :])
+            nc.vector.tensor_copy(view[:, T_HALF + SCALAR_SHARE :, :], second[:, SCALAR_SHARE:, :])
+            return pairs[:].bitcast(U32)
+
+        def quantise(grouped, width, name):
+            codes = keep.tile([P, width], U32, name=f"codes{name}", align_bytes=64)
+            scales = keep.tile([P, width], U8, name=f"scales{name}", align_bytes=64)
+            nc.vector.quantize_mx(out=codes[:].bitcast(FP8X4), scales=scales[:], in_=grouped[:])
+            return codes, scales
+
+        def multiply(acc, z, h, codes, scales):
+            cols = slice(h * P, (h + 1) * P)
+            nc.tensor.matmul_mx(
+                out=acc[:],
+                lhsT=w_codes[z][:, cols].bitcast(FP8X4),
+                lhsT_scale=w_scales[:, z, cols],
+                rhs=codes.bitcast(FP8X4),
+                rhs_scale=scales,
+                start=(z == 0),
+                stop=(z == PASSES - 1),
+            )
+
+        picked0 = keep.tile([P, 2, S], U32, name="picked0")
+        for u in range(2):
+            window = cast_pair(0, u)
+            nc.vector.tensor_copy(picked0[:, u, :], window.indirect(offsets[:]))
+        grouped0 = keep.tile([P, 4 * S], BF16, name="grouped0", align_bytes=64)
+        nc.vector.tensor_copy(
+            grouped0[:].bitcast(I32).rearrange("p (c u) -> p c u", u=2),
+            picked0[:].bitcast(I32).rearrange("p u c -> p c u"),
+        )
+        window2 = cast_pair(1, 0)
+        codes0, scales0 = quantise(grouped0, S, "0")
+
+        picked1 = [keep.tile([P, 2, CHUNK], U32, name=f"picked1_{c}") for c in range(CHUNKS)]
+        lists = [offsets[:, c * CHUNK // 16 : (c + 1) * CHUNK // 16] for c in range(CHUNKS)]
+        for c in range(CHUNKS):
+            nc.vector.tensor_copy(picked1[c][:, 0, :], window2.indirect(lists[c]))
+        window3 = cast_pair(1, 1)
+
+        accs = {}
+        for c in range(CHUNKS):
+            cols = slice(c * CHUNK, (c + 1) * CHUNK)
+            for h in range(HALVES):
+                accs[c, h] = psum.tile([P, CHUNK], F32, name="acc", tag=f"bank{HALVES * c + h}")
+                multiply(accs[c, h], 0, h, codes0[:, cols], scales0[:, cols])
+
+        grouped1 = []
+        for c in range(CHUNKS):
+            nc.vector.tensor_copy(picked1[c][:, 1, :], window3.indirect(lists[c]))
+            grouped1.append(keep.tile([P, 4 * CHUNK], BF16, name=f"grouped1_{c}", align_bytes=64))
+            nc.scalar.copy(
+                grouped1[c][:].bitcast(U32).rearrange("p (c u) -> p c u", u=2),
+                picked1[c][:].rearrange("p u c -> p c u"),
+            )
+        for c in range(CHUNKS):
+            codes1, scales1 = quantise(grouped1[c], CHUNK, f"1_{c}")
+            for h in range(HALVES):
+                multiply(accs[c, h], 1, h, codes1[:], scales1[:])
+
+        out_view = out.rearrange("(h p) j -> p h j", p=P)
+        for c in range(CHUNKS):
+            cols = slice(c * CHUNK, (c + 1) * CHUNK)
+            negated = keep.tile([P, HALVES, CHUNK], F32, name=f"negated{c}")
+            for h in range(HALVES):
+                nc.vector.scalar_tensor_tensor(
+                    negated[:, h, :], zp_picked[:, cols], csum_cols[:, h : h + 1], accs[c, h][:], MULT, SUBTRACT
+                )
+            result = keep.tile([P, HALVES, CHUNK], F32, name=f"result{c}")
+            nc.scalar.activation(result[:], negated[:], GELU, bias=zero_bias[:], scale=-1.0)
+            nc.sync.dma_start(out_view[:, :, cols], result[:])

@@ -25,7 +25,6 @@ T_HALF = T // 2
 CHUNK = 128
 CHUNKS = S // CHUNK
 SCALAR_SHARE = 176
-ZP_RUN = T // P
 
 
 def tile_picked_zeropt_gelu_l_kernel(tc, xT, zp, csum, w1_words, w1_scales, offs, out):
@@ -35,8 +34,9 @@ def tile_picked_zeropt_gelu_l_kernel(tc, xT, zp, csum, w1_words, w1_scales, offs
         psum = ctx.enter_context(tc.psum_pool(name="psum", bufs=1))
 
         offsets = keep.tile([P, S // 16], U16, name="offsets")
-        zp_runs = keep.tile([P, ZP_RUN], F32, name="zp_runs")
-        nc.scalar.dma_start(zp_runs[:], zp[0, :].rearrange("(p r) -> p r", r=ZP_RUN))
+        zp_table = keep.tile([P, T], F32, name="zp_table")
+        nc.scalar.dma_start(zp_table[P - 1 :, :], zp[0:1, :])
+        nc.vector.memset(zp_table[: P - 1, :], 0.0)
 
         raw = {}
         for z in range(PASSES):
@@ -70,24 +70,17 @@ def tile_picked_zeropt_gelu_l_kernel(tc, xT, zp, csum, w1_words, w1_scales, offs
 
         identity = keep.tile([P, P], F32, name="identity")
         make_identity(nc, identity[:])
-        zp_table = keep.tile([P, T], F32, name="zp_table")
-        zp_by_run = zp_table[:].rearrange("p (n r) -> p n r", r=ZP_RUN)
-        for b in range(2):
-            spread = psum.tile([P, 4, P], F32, name="spread", tag=f"bank{b}")
-            for r in range(4):
-                column = zp_runs[:, 4 * b + r : 4 * b + r + 1].to_broadcast([P, P])
-                nc.tensor.transpose(spread[:, r, :], column, identity[:])
-            nc.vector.tensor_copy(zp_by_run[:, :, 4 * b : 4 * b + 4], spread[:].rearrange("p r n -> p n r"))
-        zp_picked = keep.tile([P, S], F32, name="zp_picked")
-        nc.vector.tensor_copy(zp_picked[:], zp_table[:].indirect(offsets[:]))
+        zp_first = keep.tile([P, S - P], F32, name="zp_first")
+        nc.vector.tensor_copy(zp_first[:], zp_table[:].indirect(offsets[:, : (S - P) // 16]))
 
-        def cast_pair(z, u):
+        def cast_pair(z, u, share):
             pairs = keep.tile([P, 2 * T], BF16, name=f"pairs{z}{u}")
             view = pairs[:].rearrange("p (t e) -> p t e", e=2)
             first, second = (raw[z, u, h][:].rearrange("p e t -> p t e") for h in range(2))
             nc.scalar.copy(view[:, :T_HALF, :], first)
-            nc.scalar.copy(view[:, T_HALF : T_HALF + SCALAR_SHARE, :], second[:, :SCALAR_SHARE, :])
-            nc.vector.tensor_copy(view[:, T_HALF + SCALAR_SHARE :, :], second[:, SCALAR_SHARE:, :])
+            nc.scalar.copy(view[:, T_HALF : T_HALF + share, :], second[:, :share, :])
+            if share < T_HALF:
+                nc.vector.tensor_copy(view[:, T_HALF + share :, :], second[:, share:, :])
             return pairs[:].bitcast(U32)
 
         def quantise(grouped, width, name):
@@ -109,22 +102,36 @@ def tile_picked_zeropt_gelu_l_kernel(tc, xT, zp, csum, w1_words, w1_scales, offs
             )
 
         picked0 = keep.tile([P, 2, S], U32, name="picked0")
-        for u in range(2):
-            window = cast_pair(0, u)
-            nc.vector.tensor_copy(picked0[:, u, :], window.indirect(offsets[:]))
+        window0 = cast_pair(0, 0, SCALAR_SHARE)
+        nc.vector.tensor_copy(picked0[:, 0, :], window0.indirect(offsets[:]))
+        zp_second = window0.bitcast(F32)[:, :P]
+        nc.vector.tensor_copy(zp_second, zp_table[:].indirect(offsets[:, (S - P) // 16 :]))
+        turned = psum.tile([P, S // P, P], F32, name="turned", tag="bank6")
+        for b in range(S // P):
+            source = zp_first[:, b * P : (b + 1) * P] if b < S // P - 1 else zp_second
+            nc.tensor.transpose(turned[:, b, :], source, identity[:])
+        window1 = cast_pair(0, 1, SCALAR_SHARE)
+        nc.vector.tensor_copy(picked0[:, 1, :], window1.indirect(offsets[:]))
         grouped0 = keep.tile([P, 4 * S], BF16, name="grouped0", align_bytes=64)
         nc.vector.tensor_copy(
-            grouped0[:].bitcast(I32).rearrange("p (c u) -> p c u", u=2),
-            picked0[:].bitcast(I32).rearrange("p u c -> p c u"),
+            grouped0[:].bitcast(F32).rearrange("p (c u) -> p c u", u=2),
+            picked0[:].bitcast(F32).rearrange("p u c -> p c u"),
         )
-        window2 = cast_pair(1, 0)
         codes0, scales0 = quantise(grouped0, S, "0")
+        window2 = cast_pair(1, 0, T_HALF)
+        zp_cols = raw[1, 0, 0][:, 0, : S // P]
+        nc.scalar.copy(zp_cols, turned[:, :, P - 1])
+        spread = psum.tile([P, S // P, P], F32, name="spread", tag="bank7")
+        for b in range(S // P):
+            nc.tensor.transpose(spread[:, b, :], zp_cols[:, b : b + 1].to_broadcast([P, P]), identity[:])
 
         picked1 = [keep.tile([P, 2, CHUNK], U32, name=f"picked1_{c}") for c in range(CHUNKS)]
         lists = [offsets[:, c * CHUNK // 16 : (c + 1) * CHUNK // 16] for c in range(CHUNKS)]
         for c in range(CHUNKS):
             nc.vector.tensor_copy(picked1[c][:, 0, :], window2.indirect(lists[c]))
-        window3 = cast_pair(1, 1)
+        window3 = cast_pair(1, 1, T_HALF // 2)
+        zp_picked = raw[1, 1, 1][:, 0, :]
+        nc.scalar.copy(zp_picked, spread[:].rearrange("p b n -> p (b n)"))
 
         accs = {}
         for c in range(CHUNKS):

@@ -50,10 +50,8 @@ def tile_picked_zeropt_gelu_l_kernel(tc, xT, zp, csum, w1_words, w1_scales, offs
 
         w_scales = keep.tile([P, PASSES, N], U8, name="w_scales", align_bytes=64)
         nc.gpsimd.memset(w_scales[:].rearrange("p z n -> p (z n)").bitcast(I32), 0)
-        w_codes = []
-        for z in range(PASSES):
-            w_codes.append(keep.tile([P, N], U32, name=f"w_codes{z}", align_bytes=64))
-            nc.sync.dma_start(w_codes[z][:].bitcast(I32), w1_words[z].rearrange("p n t -> p (n t)").bitcast(I32))
+        w_codes = keep.tile([P, PASSES, N], U32, name="w_codes", align_bytes=64)
+        nc.sync.dma_start(w_codes[:].bitcast(I32), w1_words.rearrange("z p n t -> p z (n t)").bitcast(I32))
         for q in range(4):
             nc.sync.dma_start(
                 w_scales[32 * q : 32 * q + 4, :, :].bitcast(I32),
@@ -70,8 +68,11 @@ def tile_picked_zeropt_gelu_l_kernel(tc, xT, zp, csum, w1_words, w1_scales, offs
 
         identity = keep.tile([P, P], F32, name="identity")
         make_identity(nc, identity[:])
-        zp_first = keep.tile([P, S - P], F32, name="zp_first")
-        nc.vector.tensor_copy(zp_first[:], zp_table[:].indirect(offsets[:, : (S - P) // 16]))
+        zp_row = keep.tile([P, S], F32, name="zp_row")
+        nc.vector.tensor_copy(zp_row[:], zp_table[:].indirect(offsets[:]))
+        turned = psum.tile([P, S // P, P], F32, name="turned", tag="bank6")
+        for b in range(S // P):
+            nc.tensor.transpose(turned[:, b, :], zp_row[:, b * P : (b + 1) * P], identity[:])
 
         def cast_pair(z, u, share):
             pairs = keep.tile([P, 2 * T], BF16, name=f"pairs{z}{u}")
@@ -93,7 +94,7 @@ def tile_picked_zeropt_gelu_l_kernel(tc, xT, zp, csum, w1_words, w1_scales, offs
             cols = slice(h * P, (h + 1) * P)
             nc.tensor.matmul_mx(
                 out=acc[:],
-                lhsT=w_codes[z][:, cols].bitcast(FP8X4),
+                lhsT=w_codes[:, z, cols].bitcast(FP8X4),
                 lhsT_scale=w_scales[:, z, cols],
                 rhs=codes.bitcast(FP8X4),
                 rhs_scale=scales,
@@ -101,53 +102,48 @@ def tile_picked_zeropt_gelu_l_kernel(tc, xT, zp, csum, w1_words, w1_scales, offs
                 stop=(z == PASSES - 1),
             )
 
-        picked0 = keep.tile([P, 2, S], U32, name="picked0")
+        def columns(c, width):
+            return offsets[:, c * width // 16 : (c + 1) * width // 16]
+
+        def woven(grouped, dtype):
+            return grouped[:].bitcast(dtype).rearrange("p (c u) -> p c u", u=2)
+
+        picked0 = keep.tile([P, 2, 2, S // 2], U32, name="picked0")
         window0 = cast_pair(0, 0, SCALAR_SHARE)
-        nc.vector.tensor_copy(picked0[:, 0, :], window0.indirect(offsets[:]))
-        zp_second = window0.bitcast(F32)[:, :P]
-        nc.vector.tensor_copy(zp_second, zp_table[:].indirect(offsets[:, (S - P) // 16 :]))
-        turned = psum.tile([P, S // P, P], F32, name="turned", tag="bank6")
-        for b in range(S // P):
-            source = zp_first[:, b * P : (b + 1) * P] if b < S // P - 1 else zp_second
-            nc.tensor.transpose(turned[:, b, :], source, identity[:])
+        nc.vector.tensor_copy(picked0[:, :, 0, :], window0.indirect(offsets[:]))
         window1 = cast_pair(0, 1, SCALAR_SHARE)
-        nc.vector.tensor_copy(picked0[:, 1, :], window1.indirect(offsets[:]))
-        grouped0 = keep.tile([P, 4 * S], BF16, name="grouped0", align_bytes=64)
-        nc.vector.tensor_copy(
-            grouped0[:].bitcast(F32).rearrange("p (c u) -> p c u", u=2),
-            picked0[:].bitcast(F32).rearrange("p u c -> p c u"),
-        )
-        codes0, scales0 = quantise(grouped0, S, "0")
-        window2 = cast_pair(1, 0, T_HALF)
-        zp_cols = raw[1, 0, 0][:, 0, : S // P]
+        zp_cols = raw[0, 1, 1][:, 0, : S // P]
         nc.scalar.copy(zp_cols, turned[:, :, P - 1])
         spread = psum.tile([P, S // P, P], F32, name="spread", tag="bank7")
         for b in range(S // P):
             nc.tensor.transpose(spread[:, b, :], zp_cols[:, b : b + 1].to_broadcast([P, P]), identity[:])
+        for c in range(2):
+            nc.vector.tensor_copy(picked0[:, c, 1, :], window1.indirect(columns(c, S // 2)))
+        grouped0 = [keep.tile([P, 2 * S], BF16, name=f"grouped0_{c}", align_bytes=64) for c in range(2)]
+        for c in range(2):
+            nc.vector.tensor_copy(woven(grouped0[c], F32), picked0[:, c].bitcast(F32).rearrange("p u c -> p c u"))
+        quantised0 = [quantise(grouped0[c], S // 2, f"0_{c}") for c in range(2)]
+        window2 = cast_pair(1, 0, 400)
 
-        picked1 = [keep.tile([P, 2, CHUNK], U32, name=f"picked1_{c}") for c in range(CHUNKS)]
-        lists = [offsets[:, c * CHUNK // 16 : (c + 1) * CHUNK // 16] for c in range(CHUNKS)]
-        for c in range(CHUNKS):
-            nc.vector.tensor_copy(picked1[c][:, 0, :], window2.indirect(lists[c]))
-        window3 = cast_pair(1, 1, T_HALF // 2)
+        picked1 = keep.tile([P, CHUNKS, 2, CHUNK], U32, name="picked1")
+        nc.vector.tensor_copy(picked1[:, :, 0, :], window2.indirect(offsets[:]))
+        window3 = cast_pair(1, 1, 256)
         zp_picked = raw[1, 1, 1][:, 0, :]
         nc.scalar.copy(zp_picked, spread[:].rearrange("p b n -> p (b n)"))
 
         accs = {}
         for c in range(CHUNKS):
-            cols = slice(c * CHUNK, (c + 1) * CHUNK)
+            codes0, scales0 = quantised0[c // 2]
+            cols = slice(c % 2 * CHUNK, (c % 2 + 1) * CHUNK)
             for h in range(HALVES):
                 accs[c, h] = psum.tile([P, CHUNK], F32, name="acc", tag=f"bank{HALVES * c + h}")
                 multiply(accs[c, h], 0, h, codes0[:, cols], scales0[:, cols])
 
         grouped1 = []
         for c in range(CHUNKS):
-            nc.vector.tensor_copy(picked1[c][:, 1, :], window3.indirect(lists[c]))
+            nc.vector.tensor_copy(picked1[:, c, 1, :], window3.indirect(columns(c, CHUNK)))
             grouped1.append(keep.tile([P, 4 * CHUNK], BF16, name=f"grouped1_{c}", align_bytes=64))
-            nc.scalar.copy(
-                grouped1[c][:].bitcast(U32).rearrange("p (c u) -> p c u", u=2),
-                picked1[c][:].rearrange("p u c -> p c u"),
-            )
+            nc.scalar.copy(woven(grouped1[c], U32), picked1[:, c].rearrange("p u c -> p c u"))
         for c in range(CHUNKS):
             codes1, scales1 = quantise(grouped1[c], CHUNK, f"1_{c}")
             for h in range(HALVES):
@@ -157,10 +153,13 @@ def tile_picked_zeropt_gelu_l_kernel(tc, xT, zp, csum, w1_words, w1_scales, offs
         for c in range(CHUNKS):
             cols = slice(c * CHUNK, (c + 1) * CHUNK)
             negated = keep.tile([P, HALVES, CHUNK], F32, name=f"negated{c}")
+            result = keep.tile([P, HALVES, CHUNK], F32, name=f"result{c}")
             for h in range(HALVES):
                 nc.vector.scalar_tensor_tensor(
                     negated[:, h, :], zp_picked[:, cols], csum_cols[:, h : h + 1], accs[c, h][:], MULT, SUBTRACT
                 )
-            result = keep.tile([P, HALVES, CHUNK], F32, name=f"result{c}")
-            nc.scalar.activation(result[:], negated[:], GELU, bias=zero_bias[:], scale=-1.0)
-            nc.sync.dma_start(out_view[:, :, cols], result[:])
+                nc.scalar.activation(result[:, h, :], negated[:, h, :], GELU, bias=zero_bias[:], scale=-1.0)
+                if c == CHUNKS - 1:
+                    nc.sync.dma_start(out_view[:, h, cols], result[:, h, :])
+            if c < CHUNKS - 1:
+                nc.sync.dma_start(out_view[:, :, cols], result[:])

@@ -24,7 +24,8 @@ HALVES = N // P
 T_HALF = T // 2
 CHUNK = 128
 CHUNKS = S // CHUNK
-SCALAR_SHARE = 176
+WHOLE = [(0, 0), (0, 1)]
+SHARE = [352, 352, 512, 256]
 
 
 def tile_picked_zeropt_gelu_l_kernel(tc, xT, zp, csum, w1_words, w1_scales, offs, out):
@@ -34,6 +35,7 @@ def tile_picked_zeropt_gelu_l_kernel(tc, xT, zp, csum, w1_words, w1_scales, offs
         psum = ctx.enter_context(tc.psum_pool(name="psum", bufs=1))
 
         offsets = keep.tile([P, S // 16], U16, name="offsets")
+        nc.sync.dma_start(offsets[:], offs)
         zp_table = keep.tile([P, T], F32, name="zp_table")
         nc.scalar.dma_start(zp_table[P - 1 :, :], zp[0:1, :])
         nc.vector.memset(zp_table[: P - 1, :], 0.0)
@@ -42,11 +44,13 @@ def tile_picked_zeropt_gelu_l_kernel(tc, xT, zp, csum, w1_words, w1_scales, offs
         for z in range(PASSES):
             rows = xT[z * K_PASS : (z + 1) * K_PASS, :].rearrange("(p u e) t -> p u e t", u=2, e=2)
             for u in range(2):
-                for h in range(2):
-                    raw[z, u, h] = keep.tile([P, 2, T_HALF], F32, name=f"raw{z}{u}{h}")
-                    nc.sync.dma_start(raw[z, u, h][:], rows[:, u, :, h * T_HALF : (h + 1) * T_HALF])
-                    if (z, u, h) == (0, 0, 0):
-                        nc.sync.dma_start(offsets[:], offs)
+                if (z, u) in WHOLE:
+                    raw[z, u] = keep.tile([P, 2, T], F32, name=f"raw{z}{u}", align_bytes=64)
+                    nc.sync.dma_start(raw[z, u][:], rows[:, u, :, :])
+                else:
+                    for h in range(2):
+                        raw[z, u, h] = keep.tile([P, 2, T_HALF], F32, name=f"raw{z}{u}{h}", align_bytes=64)
+                        nc.sync.dma_start(raw[z, u, h][:], rows[:, u, :, h * T_HALF : (h + 1) * T_HALF])
 
         w_scales = keep.tile([P, PASSES, N], U8, name="w_scales", align_bytes=64)
         nc.gpsimd.memset(w_scales[:].rearrange("p z n -> p (z n)").bitcast(I32), 0)
@@ -74,20 +78,26 @@ def tile_picked_zeropt_gelu_l_kernel(tc, xT, zp, csum, w1_words, w1_scales, offs
         for b in range(S // P):
             nc.tensor.transpose(turned[:, b, :], zp_row[:, b * P : (b + 1) * P], identity[:])
 
-        def cast_pair(z, u, share):
+        def cast_pair(z, u):
+            share = SHARE[2 * z + u]
             pairs = keep.tile([P, 2 * T], BF16, name=f"pairs{z}{u}")
             view = pairs[:].rearrange("p (t e) -> p t e", e=2)
-            first, second = (raw[z, u, h][:].rearrange("p e t -> p t e") for h in range(2))
-            nc.scalar.copy(view[:, :T_HALF, :], first)
-            nc.scalar.copy(view[:, T_HALF : T_HALF + share, :], second[:, :share, :])
-            if share < T_HALF:
-                nc.vector.tensor_copy(view[:, T_HALF + share :, :], second[:, share:, :])
+            if (z, u) in WHOLE:
+                last = raw[z, u]
+            else:
+                nc.scalar.copy(view[:, :T_HALF, :], raw[z, u, 0][:].rearrange("p e t -> p t e"))
+                view = view[:, T_HALF:, :]
+                last = raw[z, u, 1]
+            source = last[:].rearrange("p e t -> p t e")
+            nc.scalar.copy(view[:, :share, :], source[:, :share, :])
+            if share < last.shape[2]:
+                nc.vector.tensor_copy(view[:, share:, :], source[:, share:, :])
             return pairs[:].bitcast(U32)
 
         def quantise(grouped, width, name):
             codes = keep.tile([P, width], U32, name=f"codes{name}", align_bytes=64)
             scales = keep.tile([P, width], U8, name=f"scales{name}", align_bytes=64)
-            nc.vector.quantize_mx(out=codes[:].bitcast(FP8X4), scales=scales[:], in_=grouped[:])
+            nc.vector.quantize_mx(out=codes[:].bitcast(FP8X4), scales=scales[:], in_=grouped)
             return codes, scales
 
         def multiply(acc, z, h, codes, scales):
@@ -106,13 +116,13 @@ def tile_picked_zeropt_gelu_l_kernel(tc, xT, zp, csum, w1_words, w1_scales, offs
             return offsets[:, c * width // 16 : (c + 1) * width // 16]
 
         def woven(grouped, dtype):
-            return grouped[:].bitcast(dtype).rearrange("p (c u) -> p c u", u=2)
+            return grouped.bitcast(dtype).rearrange("p (c u) -> p c u", u=2)
 
         picked0 = keep.tile([P, 2, 2, S // 2], U32, name="picked0")
-        window0 = cast_pair(0, 0, SCALAR_SHARE)
+        window0 = cast_pair(0, 0)
         nc.vector.tensor_copy(picked0[:, :, 0, :], window0.indirect(offsets[:]))
-        window1 = cast_pair(0, 1, SCALAR_SHARE)
-        zp_cols = raw[0, 1, 1][:, 0, : S // P]
+        window1 = cast_pair(0, 1)
+        zp_cols = raw[0, 1][:, 0, : S // P]
         nc.scalar.copy(zp_cols, turned[:, :, P - 1])
         spread = psum.tile([P, S // P, P], F32, name="spread", tag="bank7")
         for b in range(S // P):
@@ -121,13 +131,13 @@ def tile_picked_zeropt_gelu_l_kernel(tc, xT, zp, csum, w1_words, w1_scales, offs
             nc.vector.tensor_copy(picked0[:, c, 1, :], window1.indirect(columns(c, S // 2)))
         grouped0 = [keep.tile([P, 2 * S], BF16, name=f"grouped0_{c}", align_bytes=64) for c in range(2)]
         for c in range(2):
-            nc.vector.tensor_copy(woven(grouped0[c], F32), picked0[:, c].bitcast(F32).rearrange("p u c -> p c u"))
-        quantised0 = [quantise(grouped0[c], S // 2, f"0_{c}") for c in range(2)]
-        window2 = cast_pair(1, 0, 400)
+            nc.vector.tensor_copy(woven(grouped0[c][:], F32), picked0[:, c].bitcast(F32).rearrange("p u c -> p c u"))
+        quantised0 = [quantise(grouped0[c][:], S // 2, f"0_{c}") for c in range(2)]
+        window2 = cast_pair(1, 0)
 
         picked1 = keep.tile([P, CHUNKS, 2, CHUNK], U32, name="picked1")
         nc.vector.tensor_copy(picked1[:, :, 0, :], window2.indirect(offsets[:]))
-        window3 = cast_pair(1, 1, 256)
+        window3 = cast_pair(1, 1)
         zp_picked = raw[1, 1, 1][:, 0, :]
         nc.scalar.copy(zp_picked, spread[:].rearrange("p b n -> p (b n)"))
 
@@ -143,9 +153,9 @@ def tile_picked_zeropt_gelu_l_kernel(tc, xT, zp, csum, w1_words, w1_scales, offs
         for c in range(CHUNKS):
             nc.vector.tensor_copy(picked1[:, c, 1, :], window3.indirect(columns(c, CHUNK)))
             grouped1.append(keep.tile([P, 4 * CHUNK], BF16, name=f"grouped1_{c}", align_bytes=64))
-            nc.scalar.copy(woven(grouped1[c], U32), picked1[:, c].rearrange("p u c -> p c u"))
+            nc.scalar.copy(woven(grouped1[c][:], U32), picked1[:, c].rearrange("p u c -> p c u"))
         for c in range(CHUNKS):
-            codes1, scales1 = quantise(grouped1[c], CHUNK, f"1_{c}")
+            codes1, scales1 = quantise(grouped1[c][:], CHUNK, f"1_{c}")
             for h in range(HALVES):
                 multiply(accs[c, h], 1, h, codes1[:], scales1[:])
 

@@ -25,7 +25,7 @@ T_HALF = T // 2
 CHUNK = 128
 CHUNKS = S // CHUNK
 WHOLE = [(0, 0), (0, 1)]
-SHARE = [352, 352, 512, 256]
+SHARE = [352, 352, 512, 208]
 
 
 def tile_picked_zeropt_gelu_l_kernel(tc, xT, zp, csum, w1_words, w1_scales, offs, out):
@@ -38,6 +38,13 @@ def tile_picked_zeropt_gelu_l_kernel(tc, xT, zp, csum, w1_words, w1_scales, offs
         nc.sync.dma_start(offsets[:], offs)
         zp_table = keep.tile([P, T], F32, name="zp_table")
         nc.scalar.dma_start(zp_table[P - 1 :, :], zp[0:1, :])
+        w_scales = keep.tile([P, PASSES, N], U8, name="w_scales", align_bytes=64)
+        nc.vector.memset(w_scales[:].rearrange("p z n -> p (z n)").bitcast(I32), 0)
+        for q in range(4):
+            nc.scalar.dma_start(
+                w_scales[32 * q : 32 * q + 4, :, :].bitcast(I32),
+                w1_scales[:, 4 * q : 4 * q + 4, :].rearrange("z r n -> r z n").bitcast(I32),
+            )
         nc.vector.memset(zp_table[: P - 1, :], 0.0)
 
         raw = {}
@@ -52,15 +59,9 @@ def tile_picked_zeropt_gelu_l_kernel(tc, xT, zp, csum, w1_words, w1_scales, offs
                         raw[z, u, h] = keep.tile([P, 2, T_HALF], F32, name=f"raw{z}{u}{h}", align_bytes=64)
                         nc.sync.dma_start(raw[z, u, h][:], rows[:, u, :, h * T_HALF : (h + 1) * T_HALF])
 
-        w_scales = keep.tile([P, PASSES, N], U8, name="w_scales", align_bytes=64)
-        nc.gpsimd.memset(w_scales[:].rearrange("p z n -> p (z n)").bitcast(I32), 0)
-        w_codes = keep.tile([P, PASSES, N], U32, name="w_codes", align_bytes=64)
-        nc.sync.dma_start(w_codes[:].bitcast(I32), w1_words.rearrange("z p n t -> p z (n t)").bitcast(I32))
-        for q in range(4):
-            nc.sync.dma_start(
-                w_scales[32 * q : 32 * q + 4, :, :].bitcast(I32),
-                w1_scales[:, 4 * q : 4 * q + 4, :].rearrange("z r n -> r z n").bitcast(I32),
-            )
+        w_codes = [keep.tile([P, N], U32, name=f"w_codes{z}", align_bytes=64) for z in range(PASSES)]
+        for z in range(PASSES):
+            nc.sync.dma_start(w_codes[z][:].bitcast(I32), w1_words[z].rearrange("p n t -> p (n t)").bitcast(I32))
         csum_cols = keep.tile([P, HALVES], F32, name="csum_cols")
         with nc.allow_non_contiguous_dma(reason="one value to a partition"):
             nc.sync.dma_start(csum_cols[:], csum.rearrange("(h p) o -> p (h o)", p=P))
@@ -104,7 +105,7 @@ def tile_picked_zeropt_gelu_l_kernel(tc, xT, zp, csum, w1_words, w1_scales, offs
             cols = slice(h * P, (h + 1) * P)
             nc.tensor.matmul_mx(
                 out=acc[:],
-                lhsT=w_codes[:, z, cols].bitcast(FP8X4),
+                lhsT=w_codes[z][:, cols].bitcast(FP8X4),
                 lhsT_scale=w_scales[:, z, cols],
                 rhs=codes.bitcast(FP8X4),
                 rhs_scale=scales,
@@ -159,10 +160,11 @@ def tile_picked_zeropt_gelu_l_kernel(tc, xT, zp, csum, w1_words, w1_scales, offs
             for h in range(HALVES):
                 multiply(accs[c, h], 1, h, codes1[:], scales1[:])
 
+        differences = keep.tile([P, CHUNKS, HALVES, CHUNK], F32, name="differences", tag="picked1")
         out_view = out.rearrange("(h p) j -> p h j", p=P)
         for c in range(CHUNKS):
             cols = slice(c * CHUNK, (c + 1) * CHUNK)
-            negated = keep.tile([P, HALVES, CHUNK], F32, name=f"negated{c}")
+            negated = differences[:, c]
             result = keep.tile([P, HALVES, CHUNK], F32, name=f"result{c}")
             for h in range(HALVES):
                 nc.vector.scalar_tensor_tensor(

@@ -139,9 +139,17 @@ def tile_picked_zeropt_gelu_l_kernel(tc, xT, zp, csum, w1_words, w1_scales, offs
         picked1 = keep.tile([P, CHUNKS, 2, CHUNK], U32, name="picked1")
         nc.vector.tensor_copy(picked1[:, :, 0, :], window2.indirect(offsets[:]))
         window3 = cast_pair(1, 1)
-        zp_picked = raw[1, 1, 1][:, 0, :]
-        nc.scalar.copy(zp_picked, spread[:].rearrange("p b n -> p (b n)"))
+        zp_picked = [raw[1, 1, 1][:, 0, : S // 2]]
+        nc.scalar.copy(zp_picked[0], spread[:, :2, :].rearrange("p b n -> p (b n)"))
 
+        grouped1 = []
+        for c in range(CHUNKS):
+            nc.vector.tensor_copy(picked1[:, c, 1, :], window3.indirect(columns(c, CHUNK)))
+            grouped1.append(keep.tile([P, 4 * CHUNK], BF16, name=f"grouped1_{c}", align_bytes=64))
+            nc.scalar.copy(woven(grouped1[c][:], U32), picked1[:, c].rearrange("p u c -> p c u"))
+        zp_late = keep.tile([P, S // 2], F32, name="zp_late", tag="pairs11")
+        zp_picked.append(zp_late[:])
+        nc.scalar.copy(zp_picked[1], spread[:, 2:, :].rearrange("p b n -> p (b n)"))
         accs = {}
         for c in range(CHUNKS):
             codes0, scales0 = quantised0[c // 2]
@@ -150,11 +158,6 @@ def tile_picked_zeropt_gelu_l_kernel(tc, xT, zp, csum, w1_words, w1_scales, offs
                 accs[c, h] = psum.tile([P, CHUNK], F32, name="acc", tag=f"bank{HALVES * c + h}")
                 multiply(accs[c, h], 0, h, codes0[:, cols], scales0[:, cols])
 
-        grouped1 = []
-        for c in range(CHUNKS):
-            nc.vector.tensor_copy(picked1[:, c, 1, :], window3.indirect(columns(c, CHUNK)))
-            grouped1.append(keep.tile([P, 4 * CHUNK], BF16, name=f"grouped1_{c}", align_bytes=64))
-            nc.scalar.copy(woven(grouped1[c][:], U32), picked1[:, c].rearrange("p u c -> p c u"))
         for c in range(CHUNKS):
             codes1, scales1 = quantise(grouped1[c][:], CHUNK, f"1_{c}")
             for h in range(HALVES):
@@ -168,10 +171,10 @@ def tile_picked_zeropt_gelu_l_kernel(tc, xT, zp, csum, w1_words, w1_scales, offs
             result = keep.tile([P, HALVES, CHUNK], F32, name=f"result{c}")
             for h in range(HALVES):
                 nc.vector.scalar_tensor_tensor(
-                    negated[:, h, :], zp_picked[:, cols], csum_cols[:, h : h + 1], accs[c, h][:], MULT, SUBTRACT
+                    negated[:, h, :], zp_picked[c // 2][:, c % 2 * CHUNK : (c % 2 + 1) * CHUNK], csum_cols[:, h : h + 1], accs[c, h][:], MULT, SUBTRACT
                 )
                 nc.scalar.activation(result[:, h, :], negated[:, h, :], GELU, bias=zero_bias[:], scale=-1.0)
-                if c == CHUNKS - 1:
+                if c in (0, CHUNKS - 1):
                     nc.sync.dma_start(out_view[:, h, cols], result[:, h, :])
-            if c < CHUNKS - 1:
+            if c not in (0, CHUNKS - 1):
                 nc.sync.dma_start(out_view[:, :, cols], result[:])

@@ -15,6 +15,7 @@ U8 = mybir.dt.uint8
 FP8X4 = mybir.dt.float8_e4m3fn_x4
 GELU = mybir.ActivationFunctionType.Gelu_apprx_tanh
 MULT = mybir.AluOpType.mult
+ADD = mybir.AluOpType.add
 SUBTRACT = mybir.AluOpType.subtract
 
 P = 128
@@ -24,8 +25,10 @@ HALVES = N // P
 T_HALF = T // 2
 CHUNK = 128
 CHUNKS = S // CHUNK
-WHOLE = [(0, 0), (0, 1)]
-SHARE = [352, 352, 512, 208]
+HALVED = []
+CUT = [1024, 1024, 512, 512]
+SHARE = [352, 352, 1024, 0]
+POOL_SHARE = 208
 
 
 def tile_picked_zeropt_gelu_l_kernel(tc, xT, zp, csum, w1_words, w1_scales, offs, out):
@@ -51,13 +54,17 @@ def tile_picked_zeropt_gelu_l_kernel(tc, xT, zp, csum, w1_words, w1_scales, offs
         for z in range(PASSES):
             rows = xT[z * K_PASS : (z + 1) * K_PASS, :].rearrange("(p u e) t -> p u e t", u=2, e=2)
             for u in range(2):
-                if (z, u) in WHOLE:
-                    raw[z, u] = keep.tile([P, 2, T], F32, name=f"raw{z}{u}", align_bytes=64)
-                    nc.sync.dma_start(raw[z, u][:], rows[:, u, :, :])
-                else:
+                if (z, u) in HALVED:
                     for h in range(2):
                         raw[z, u, h] = keep.tile([P, 2, T_HALF], F32, name=f"raw{z}{u}{h}", align_bytes=64)
                         nc.sync.dma_start(raw[z, u, h][:], rows[:, u, :, h * T_HALF : (h + 1) * T_HALF])
+                else:
+                    raw[z, u] = keep.tile([P, 2 * T], F32, name=f"raw{z}{u}", align_bytes=64)
+                    run = rows[:, u, :, :].rearrange("p e t -> p (e t)")
+                    cut = T + CUT[2 * z + u]
+                    nc.sync.dma_start(raw[z, u][:, :cut], run[:, :cut])
+                    if cut < 2 * T:
+                        nc.sync.dma_start(raw[z, u][:, cut:], run[:, cut:])
 
         w_codes = [keep.tile([P, N], U32, name=f"w_codes{z}", align_bytes=64) for z in range(PASSES)]
         for z in range(PASSES):
@@ -83,15 +90,18 @@ def tile_picked_zeropt_gelu_l_kernel(tc, xT, zp, csum, w1_words, w1_scales, offs
             share = SHARE[2 * z + u]
             pairs = keep.tile([P, 2 * T], BF16, name=f"pairs{z}{u}")
             view = pairs[:].rearrange("p (t e) -> p t e", e=2)
-            if (z, u) in WHOLE:
-                last = raw[z, u]
-            else:
+            if (z, u) in HALVED:
                 nc.scalar.copy(view[:, :T_HALF, :], raw[z, u, 0][:].rearrange("p e t -> p t e"))
                 view = view[:, T_HALF:, :]
-                last = raw[z, u, 1]
-            source = last[:].rearrange("p e t -> p t e")
-            nc.scalar.copy(view[:, :share, :], source[:, :share, :])
-            if share < last.shape[2]:
+                source = raw[z, u, 1][:].rearrange("p e t -> p t e")
+                done = 0
+            else:
+                source = raw[z, u][:].rearrange("p (e t) -> p t e", e=2)
+                done = min(share, CUT[2 * z + u])
+                nc.scalar.copy(view[:, :done, :], source[:, :done, :])
+            if done < share:
+                nc.scalar.copy(view[:, done:share, :], source[:, done:share, :])
+            if share < source.shape[1]:
                 nc.vector.tensor_copy(view[:, share:, :], source[:, share:, :])
             return pairs[:].bitcast(U32)
 
@@ -123,7 +133,7 @@ def tile_picked_zeropt_gelu_l_kernel(tc, xT, zp, csum, w1_words, w1_scales, offs
         window0 = cast_pair(0, 0)
         nc.vector.tensor_copy(picked0[:, :, 0, :], window0.indirect(offsets[:]))
         window1 = cast_pair(0, 1)
-        zp_cols = raw[0, 1][:, 0, : S // P]
+        zp_cols = raw[0, 1][:, : S // P]
         nc.scalar.copy(zp_cols, turned[:, :, P - 1])
         spread = psum.tile([P, S // P, P], F32, name="spread", tag="bank7")
         for b in range(S // P):
@@ -138,8 +148,15 @@ def tile_picked_zeropt_gelu_l_kernel(tc, xT, zp, csum, w1_words, w1_scales, offs
 
         picked1 = keep.tile([P, CHUNKS, 2, CHUNK], U32, name="picked1")
         nc.vector.tensor_copy(picked1[:, :, 0, :], window2.indirect(offsets[:]))
-        window3 = cast_pair(1, 1)
-        zp_picked = [raw[1, 1, 1][:, 0, : S // 2]]
+        pairs3 = keep.tile([P, 2 * T], BF16, name="pairs11")
+        view3 = pairs3[:].rearrange("p (t e) -> p t e", e=2)
+        source3 = raw[1, 1][:].rearrange("p (e t) -> p t e", e=2)
+        for lo, hi in ((0, CUT[3]), (CUT[3], T)):
+            mid = hi - POOL_SHARE
+            nc.scalar.copy(view3[:, lo:mid, :], source3[:, lo:mid, :])
+            nc.gpsimd.tensor_scalar(view3[:, mid:hi, :], source3[:, mid:hi, :], 1.0, 0.0, MULT, ADD)
+        window3 = pairs3[:].bitcast(U32)
+        zp_picked = [raw[1, 1][:, T_HALF : T_HALF + S // 2]]
         nc.scalar.copy(zp_picked[0], spread[:, :2, :].rearrange("p b n -> p (b n)"))
 
         grouped1 = []

@@ -26,9 +26,9 @@ T_HALF = T // 2
 CHUNK = 128
 CHUNKS = S // CHUNK
 HALVED = []
-CUT = [1024, 1024, 512, 512]
+CUT = [1024, 1024, 384, 512]
 SHARE = [352, 352, 1024, 0]
-POOL_SHARE = 208
+POOL_SHARE = [232, 232]
 
 
 def tile_picked_zeropt_gelu_l_kernel(tc, xT, zp, csum, w1_words, w1_scales, offs, out):
@@ -151,8 +151,8 @@ def tile_picked_zeropt_gelu_l_kernel(tc, xT, zp, csum, w1_words, w1_scales, offs
         pairs3 = keep.tile([P, 2 * T], BF16, name="pairs11")
         view3 = pairs3[:].rearrange("p (t e) -> p t e", e=2)
         source3 = raw[1, 1][:].rearrange("p (e t) -> p t e", e=2)
-        for lo, hi in ((0, CUT[3]), (CUT[3], T)):
-            mid = hi - POOL_SHARE
+        for lo, hi, pool_share in ((0, CUT[3], POOL_SHARE[0]), (CUT[3], T, POOL_SHARE[1])):
+            mid = hi - pool_share
             nc.scalar.copy(view3[:, lo:mid, :], source3[:, lo:mid, :])
             nc.gpsimd.tensor_scalar(view3[:, mid:hi, :], source3[:, mid:hi, :], 1.0, 0.0, MULT, ADD)
         window3 = pairs3[:].bitcast(U32)

@@ -22,13 +22,14 @@ P = 128
 K_PASS = 512
 PASSES = K // K_PASS
 HALVES = N // P
-T_HALF = T // 2
 CHUNK = 128
 CHUNKS = S // CHUNK
-HALVED = []
-CUT = [1024, 1024, 384, 512]
-SHARE = [352, 352, 1024, 0]
-POOL_SHARE = [232, 232]
+WIDE = S // 2
+BLOCKS = S // P
+
+SCALAR_SHARE = 352
+CUTS = [384, 512]
+GPSIMD_SHARE = 224
 
 
 def tile_picked_zeropt_gelu_l_kernel(tc, xT, zp, csum, w1_words, w1_scales, offs, out):
@@ -40,31 +41,31 @@ def tile_picked_zeropt_gelu_l_kernel(tc, xT, zp, csum, w1_words, w1_scales, offs
         offsets = keep.tile([P, S // 16], U16, name="offsets")
         nc.sync.dma_start(offsets[:], offs)
         zp_table = keep.tile([P, T], F32, name="zp_table")
-        nc.scalar.dma_start(zp_table[P - 1 :, :], zp[0:1, :])
+
+        raw = {}
+        runs = {}
+        for z in range(PASSES):
+            for u in range(2):
+                raw[z, u] = keep.tile([P, 2 * T], F32, name=f"raw{z}{u}", align_bytes=64)
+                runs[z, u] = xT[z * K_PASS : (z + 1) * K_PASS, :].rearrange("(p u e) t -> p u (e t)", u=2, e=2)[:, u, :]
+
+        nc.scalar.dma_start(raw[0, 0][0:P:2, :], runs[0, 0][0:P:2, :])
+        nc.sync.dma_start(zp_table[P - 1 :, :], zp[0:1, :])
+        nc.sync.dma_start(raw[0, 0][1:P:2, :], runs[0, 0][1:P:2, :])
+        nc.sync.dma_start(raw[0, 1][:], runs[0, 1])
+
         w_scales = keep.tile([P, PASSES, N], U8, name="w_scales", align_bytes=64)
         nc.vector.memset(w_scales[:].rearrange("p z n -> p (z n)").bitcast(I32), 0)
         for q in range(4):
-            nc.scalar.dma_start(
+            nc.sync.dma_start(
                 w_scales[32 * q : 32 * q + 4, :, :].bitcast(I32),
                 w1_scales[:, 4 * q : 4 * q + 4, :].rearrange("z r n -> r z n").bitcast(I32),
             )
         nc.vector.memset(zp_table[: P - 1, :], 0.0)
-
-        raw = {}
-        for z in range(PASSES):
-            rows = xT[z * K_PASS : (z + 1) * K_PASS, :].rearrange("(p u e) t -> p u e t", u=2, e=2)
-            for u in range(2):
-                if (z, u) in HALVED:
-                    for h in range(2):
-                        raw[z, u, h] = keep.tile([P, 2, T_HALF], F32, name=f"raw{z}{u}{h}", align_bytes=64)
-                        nc.sync.dma_start(raw[z, u, h][:], rows[:, u, :, h * T_HALF : (h + 1) * T_HALF])
-                else:
-                    raw[z, u] = keep.tile([P, 2 * T], F32, name=f"raw{z}{u}", align_bytes=64)
-                    run = rows[:, u, :, :].rearrange("p e t -> p (e t)")
-                    cut = T + CUT[2 * z + u]
-                    nc.sync.dma_start(raw[z, u][:, :cut], run[:, :cut])
-                    if cut < 2 * T:
-                        nc.sync.dma_start(raw[z, u][:, cut:], run[:, cut:])
+        for u in range(2):
+            cut = T + CUTS[u]
+            nc.sync.dma_start(raw[1, u][:, :cut], runs[1, u][:, :cut])
+            nc.sync.dma_start(raw[1, u][:, cut:], runs[1, u][:, cut:])
 
         w_codes = [keep.tile([P, N], U32, name=f"w_codes{z}", align_bytes=64) for z in range(PASSES)]
         for z in range(PASSES):
@@ -82,27 +83,18 @@ def tile_picked_zeropt_gelu_l_kernel(tc, xT, zp, csum, w1_words, w1_scales, offs
         make_identity(nc, identity[:])
         zp_row = keep.tile([P, S], F32, name="zp_row")
         nc.vector.tensor_copy(zp_row[:], zp_table[:].indirect(offsets[:]))
-        turned = psum.tile([P, S // P, P], F32, name="turned", tag="bank6")
-        for b in range(S // P):
+        turned = psum.tile([P, BLOCKS, P], F32, name="turned", tag="bank6")
+        for b in range(BLOCKS):
             nc.tensor.transpose(turned[:, b, :], zp_row[:, b * P : (b + 1) * P], identity[:])
 
-        def cast_pair(z, u):
-            share = SHARE[2 * z + u]
+        def pair_views(z, u):
             pairs = keep.tile([P, 2 * T], BF16, name=f"pairs{z}{u}")
-            view = pairs[:].rearrange("p (t e) -> p t e", e=2)
-            if (z, u) in HALVED:
-                nc.scalar.copy(view[:, :T_HALF, :], raw[z, u, 0][:].rearrange("p e t -> p t e"))
-                view = view[:, T_HALF:, :]
-                source = raw[z, u, 1][:].rearrange("p e t -> p t e")
-                done = 0
-            else:
-                source = raw[z, u][:].rearrange("p (e t) -> p t e", e=2)
-                done = min(share, CUT[2 * z + u])
-                nc.scalar.copy(view[:, :done, :], source[:, :done, :])
-            if done < share:
-                nc.scalar.copy(view[:, done:share, :], source[:, done:share, :])
-            if share < source.shape[1]:
-                nc.vector.tensor_copy(view[:, share:, :], source[:, share:, :])
+            return pairs, pairs[:].rearrange("p (t e) -> p t e", e=2), raw[z, u][:].rearrange("p (e t) -> p t e", e=2)
+
+        def cast_whole(u):
+            pairs, target, source = pair_views(0, u)
+            nc.scalar.copy(target[:, :SCALAR_SHARE, :], source[:, :SCALAR_SHARE, :])
+            nc.vector.tensor_copy(target[:, SCALAR_SHARE:, :], source[:, SCALAR_SHARE:, :])
             return pairs[:].bitcast(U32)
 
         def quantise(grouped, width, name):
@@ -112,86 +104,86 @@ def tile_picked_zeropt_gelu_l_kernel(tc, xT, zp, csum, w1_words, w1_scales, offs
             return codes, scales
 
         def multiply(acc, z, h, codes, scales):
-            cols = slice(h * P, (h + 1) * P)
+            channels = slice(h * P, (h + 1) * P)
             nc.tensor.matmul_mx(
                 out=acc[:],
-                lhsT=w_codes[z][:, cols].bitcast(FP8X4),
-                lhsT_scale=w_scales[:, z, cols],
+                lhsT=w_codes[z][:, channels].bitcast(FP8X4),
+                lhsT_scale=w_scales[:, z, channels],
                 rhs=codes.bitcast(FP8X4),
                 rhs_scale=scales,
                 start=(z == 0),
                 stop=(z == PASSES - 1),
             )
 
-        def columns(c, width):
+        def entries(c, width):
             return offsets[:, c * width // 16 : (c + 1) * width // 16]
 
         def woven(grouped, dtype):
-            return grouped.bitcast(dtype).rearrange("p (c u) -> p c u", u=2)
+            return grouped.bitcast(dtype).rearrange("p (n u) -> p n u", u=2)
 
-        picked0 = keep.tile([P, 2, 2, S // 2], U32, name="picked0")
-        window0 = cast_pair(0, 0)
-        nc.vector.tensor_copy(picked0[:, :, 0, :], window0.indirect(offsets[:]))
-        window1 = cast_pair(0, 1)
-        zp_cols = raw[0, 1][:, : S // P]
+        picked0 = keep.tile([P, 2, 2, WIDE], U32, name="picked0")
+        nc.vector.tensor_copy(picked0[:, :, 0, :], cast_whole(0).indirect(offsets[:]))
+        window = cast_whole(1)
+        zp_cols = raw[0, 1][:, :BLOCKS]
         nc.scalar.copy(zp_cols, turned[:, :, P - 1])
-        spread = psum.tile([P, S // P, P], F32, name="spread", tag="bank7")
-        for b in range(S // P):
+        spread = psum.tile([P, BLOCKS, P], F32, name="spread", tag="bank7")
+        for b in range(BLOCKS):
             nc.tensor.transpose(spread[:, b, :], zp_cols[:, b : b + 1].to_broadcast([P, P]), identity[:])
         for c in range(2):
-            nc.vector.tensor_copy(picked0[:, c, 1, :], window1.indirect(columns(c, S // 2)))
-        grouped0 = [keep.tile([P, 2 * S], BF16, name=f"grouped0_{c}", align_bytes=64) for c in range(2)]
+            nc.vector.tensor_copy(picked0[:, c, 1, :], window.indirect(entries(c, WIDE)))
+        grouped0 = [keep.tile([P, 4 * WIDE], BF16, name=f"grouped0_{c}", align_bytes=64) for c in range(2)]
         for c in range(2):
-            nc.vector.tensor_copy(woven(grouped0[c][:], F32), picked0[:, c].bitcast(F32).rearrange("p u c -> p c u"))
-        quantised0 = [quantise(grouped0[c][:], S // 2, f"0_{c}") for c in range(2)]
-        window2 = cast_pair(1, 0)
+            nc.vector.tensor_copy(woven(grouped0[c][:], F32), picked0[:, c].bitcast(F32).rearrange("p u n -> p n u"))
+        quantised0 = [quantise(grouped0[c][:], WIDE, f"0_{c}") for c in range(2)]
 
+        pairs10, target, source = pair_views(1, 0)
+        for lo, hi in ((0, CUTS[0]), (CUTS[0], T)):
+            nc.scalar.copy(target[:, lo:hi, :], source[:, lo:hi, :])
         picked1 = keep.tile([P, CHUNKS, 2, CHUNK], U32, name="picked1")
-        nc.vector.tensor_copy(picked1[:, :, 0, :], window2.indirect(offsets[:]))
-        pairs3 = keep.tile([P, 2 * T], BF16, name="pairs11")
-        view3 = pairs3[:].rearrange("p (t e) -> p t e", e=2)
-        source3 = raw[1, 1][:].rearrange("p (e t) -> p t e", e=2)
-        for lo, hi, pool_share in ((0, CUT[3], POOL_SHARE[0]), (CUT[3], T, POOL_SHARE[1])):
-            mid = hi - pool_share
-            nc.scalar.copy(view3[:, lo:mid, :], source3[:, lo:mid, :])
-            nc.gpsimd.tensor_scalar(view3[:, mid:hi, :], source3[:, mid:hi, :], 1.0, 0.0, MULT, ADD)
-        window3 = pairs3[:].bitcast(U32)
-        zp_picked = [raw[1, 1][:, T_HALF : T_HALF + S // 2]]
-        nc.scalar.copy(zp_picked[0], spread[:, :2, :].rearrange("p b n -> p (b n)"))
+        nc.vector.tensor_copy(picked1[:, :, 0, :], pairs10[:].bitcast(U32).indirect(offsets[:]))
 
+        pairs11, target, source = pair_views(1, 1)
+        for lo, hi in ((0, CUTS[1]), (CUTS[1], T)):
+            mid = hi - GPSIMD_SHARE
+            nc.scalar.copy(target[:, lo:mid, :], source[:, lo:mid, :])
+            nc.gpsimd.tensor_scalar(target[:, mid:hi, :], source[:, mid:hi, :], 1.0, 0.0, MULT, ADD)
+        window = pairs11[:].bitcast(U32)
+
+        zp_picked = [raw[1, 1][:, CUTS[1] : CUTS[1] + WIDE]]
+        nc.scalar.copy(zp_picked[0], spread[:, : BLOCKS // 2, :].rearrange("p b n -> p (b n)"))
         grouped1 = []
         for c in range(CHUNKS):
-            nc.vector.tensor_copy(picked1[:, c, 1, :], window3.indirect(columns(c, CHUNK)))
+            nc.vector.tensor_copy(picked1[:, c, 1, :], window.indirect(entries(c, CHUNK)))
             grouped1.append(keep.tile([P, 4 * CHUNK], BF16, name=f"grouped1_{c}", align_bytes=64))
-            nc.scalar.copy(woven(grouped1[c][:], U32), picked1[:, c].rearrange("p u c -> p c u"))
-        zp_late = keep.tile([P, S // 2], F32, name="zp_late", tag="pairs11")
+            nc.scalar.copy(woven(grouped1[c][:], U32), picked1[:, c].rearrange("p u n -> p n u"))
+        zp_late = keep.tile([P, WIDE], F32, name="zp_late", tag="pairs11")
         zp_picked.append(zp_late[:])
-        nc.scalar.copy(zp_picked[1], spread[:, 2:, :].rearrange("p b n -> p (b n)"))
+        nc.scalar.copy(zp_picked[1], spread[:, BLOCKS // 2 :, :].rearrange("p b n -> p (b n)"))
+
         accs = {}
         for c in range(CHUNKS):
-            codes0, scales0 = quantised0[c // 2]
-            cols = slice(c % 2 * CHUNK, (c % 2 + 1) * CHUNK)
+            codes, scales = quantised0[c * CHUNK // WIDE]
+            cols = slice(c * CHUNK % WIDE, c * CHUNK % WIDE + CHUNK)
             for h in range(HALVES):
                 accs[c, h] = psum.tile([P, CHUNK], F32, name="acc", tag=f"bank{HALVES * c + h}")
-                multiply(accs[c, h], 0, h, codes0[:, cols], scales0[:, cols])
-
+                multiply(accs[c, h], 0, h, codes[:, cols], scales[:, cols])
         for c in range(CHUNKS):
-            codes1, scales1 = quantise(grouped1[c][:], CHUNK, f"1_{c}")
+            codes, scales = quantise(grouped1[c][:], CHUNK, f"1_{c}")
             for h in range(HALVES):
-                multiply(accs[c, h], 1, h, codes1[:], scales1[:])
+                multiply(accs[c, h], 1, h, codes[:], scales[:])
 
         differences = keep.tile([P, CHUNKS, HALVES, CHUNK], F32, name="differences", tag="picked1")
         out_view = out.rearrange("(h p) j -> p h j", p=P)
         for c in range(CHUNKS):
             cols = slice(c * CHUNK, (c + 1) * CHUNK)
-            negated = differences[:, c]
+            zp_chunk = zp_picked[c * CHUNK // WIDE][:, c * CHUNK % WIDE : c * CHUNK % WIDE + CHUNK]
             result = keep.tile([P, HALVES, CHUNK], F32, name=f"result{c}")
+            by_halves = c in (0, CHUNKS - 1)
             for h in range(HALVES):
-                nc.vector.scalar_tensor_tensor(
-                    negated[:, h, :], zp_picked[c // 2][:, c % 2 * CHUNK : (c % 2 + 1) * CHUNK], csum_cols[:, h : h + 1], accs[c, h][:], MULT, SUBTRACT
-                )
-                nc.scalar.activation(result[:, h, :], negated[:, h, :], GELU, bias=zero_bias[:], scale=-1.0)
-                if c in (0, CHUNKS - 1):
+                negated = differences[:, c, h, :]
+                nc.vector.scalar_tensor_tensor(negated, zp_chunk, csum_cols[:, h : h + 1], accs[c, h][:], MULT, SUBTRACT)
+                nc.scalar.activation(result[:, h, :], negated, GELU, bias=zero_bias[:], scale=-1.0)
+                if by_halves:
                     nc.sync.dma_start(out_view[:, h, cols], result[:, h, :])
-            if c not in (0, CHUNKS - 1):
+            if not by_halves:
                 nc.sync.dma_start(out_view[:, :, cols], result[:])

@@ -14,22 +14,17 @@ U16 = mybir.dt.uint16
 U8 = mybir.dt.uint8
 FP8X4 = mybir.dt.float8_e4m3fn_x4
 GELU = mybir.ActivationFunctionType.Gelu_apprx_tanh
+COPY = mybir.ActivationFunctionType.Copy
 MULT = mybir.AluOpType.mult
-ADD = mybir.AluOpType.add
 SUBTRACT = mybir.AluOpType.subtract
 
 P = 128
-K_PASS = 512
+PACK = 4
+K_PASS = P * PACK
 PASSES = K // K_PASS
 HALVES = N // P
 CHUNK = 128
 CHUNKS = S // CHUNK
-WIDE = S // 2
-BLOCKS = S // P
-
-SCALAR_SHARE = 352
-CUTS = [384, 512]
-GPSIMD_SHARE = 224
 
 
 def tile_picked_zeropt_gelu_l_kernel(tc, xT, zp, csum, w1_words, w1_scales, offs, out):
@@ -41,18 +36,23 @@ def tile_picked_zeropt_gelu_l_kernel(tc, xT, zp, csum, w1_words, w1_scales, offs
         offsets = keep.tile([P, S // 16], U16, name="offsets")
         nc.sync.dma_start(offsets[:], offs)
         zp_table = keep.tile([P, T], F32, name="zp_table")
+        csum_rows = keep.tile([P, P], F32, name="csum_rows")
 
-        raw = {}
-        runs = {}
+        rows = {}
         for z in range(PASSES):
-            for u in range(2):
-                raw[z, u] = keep.tile([P, 2 * T], F32, name=f"raw{z}{u}", align_bytes=64)
-                runs[z, u] = xT[z * K_PASS : (z + 1) * K_PASS, :].rearrange("(p u e) t -> p u (e t)", u=2, e=2)[:, u, :]
+            for t in range(PACK):
+                rows[z, t] = keep.tile([P, T], F32, name=f"row{z}{t}", align_bytes=64)
 
-        nc.scalar.dma_start(raw[0, 0][0:P:2, :], runs[0, 0][0:P:2, :])
+        def load_row(queue, z, t, parts=slice(0, P)):
+            source = xT[z * K_PASS : (z + 1) * K_PASS, :].rearrange("(p t) n -> p t n", t=PACK)
+            queue.dma_start(rows[z, t][parts, :], source[parts, t, :])
+
+        load_row(nc.scalar, 0, 0, slice(0, P, 2))
         nc.sync.dma_start(zp_table[P - 1 :, :], zp[0:1, :])
-        nc.sync.dma_start(raw[0, 0][1:P:2, :], runs[0, 0][1:P:2, :])
-        nc.sync.dma_start(raw[0, 1][:], runs[0, 1])
+        nc.sync.dma_start(csum_rows[P - HALVES :, :], csum.rearrange("(h p) o -> h (p o)", p=P))
+        load_row(nc.sync, 0, 0, slice(1, P, 2))
+        for t in range(1, PACK):
+            load_row(nc.sync, 0, t)
 
         w_scales = keep.tile([P, PASSES, N], U8, name="w_scales", align_bytes=64)
         nc.vector.memset(w_scales[:].rearrange("p z n -> p (z n)").bitcast(I32), 0)
@@ -62,128 +62,143 @@ def tile_picked_zeropt_gelu_l_kernel(tc, xT, zp, csum, w1_words, w1_scales, offs
                 w1_scales[:, 4 * q : 4 * q + 4, :].rearrange("z r n -> r z n").bitcast(I32),
             )
         nc.vector.memset(zp_table[: P - 1, :], 0.0)
-        for u in range(2):
-            cut = T + CUTS[u]
-            nc.sync.dma_start(raw[1, u][:, :cut], runs[1, u][:, :cut])
-            nc.sync.dma_start(raw[1, u][:, cut:], runs[1, u][:, cut:])
+        nc.vector.memset(csum_rows[: P - HALVES, :], 0.0)
+        for t in range(PACK):
+            load_row(nc.sync, 1, t)
 
         w_codes = [keep.tile([P, N], U32, name=f"w_codes{z}", align_bytes=64) for z in range(PASSES)]
         for z in range(PASSES):
             nc.sync.dma_start(w_codes[z][:].bitcast(I32), w1_words[z].rearrange("p n t -> p (n t)").bitcast(I32))
-        csum_cols = keep.tile([P, HALVES], F32, name="csum_cols")
-        with nc.allow_non_contiguous_dma(reason="one value to a partition"):
-            nc.sync.dma_start(csum_cols[:], csum.rearrange("(h p) o -> p (h o)", p=P))
 
         zero_in = keep.tile([P, 1], F32, name="zero_in")
         zero_bias = keep.tile([P, 1], F32, name="zero_bias")
         nc.vector.memset(zero_in[:], 0.0)
         nc.scalar.activation(zero_bias[:], zero_in[:], GELU)
 
+        def entries(lo, hi):
+            return offsets[:, lo * CHUNK // 16 : hi * CHUNK // 16]
+
+        def tokens(lo, hi):
+            return slice(lo * CHUNK, hi * CHUNK)
+
+        grouped = {}
+        for z in range(PASSES):
+            for c in range(CHUNKS):
+                grouped[z, c] = keep.tile([P, CHUNK, PACK], BF16, name=f"grouped{z}{c}", align_bytes=64)
+        early0 = keep.tile([P, 2, S], BF16, name="early0")
+        early1 = keep.tile([P, 2, S - CHUNK], BF16, name="early1")
+        late = {}
+        for z in range(PASSES):
+            for c in range(1, CHUNKS):
+                late[z, c] = keep.tile([P, 2, CHUNK], BF16, name=f"late{z}{c}")
+
         identity = keep.tile([P, P], F32, name="identity")
         make_identity(nc, identity[:])
         zp_row = keep.tile([P, S], F32, name="zp_row")
-        nc.vector.tensor_copy(zp_row[:], zp_table[:].indirect(offsets[:]))
-        turned = psum.tile([P, BLOCKS, P], F32, name="turned", tag="bank6")
-        for b in range(BLOCKS):
-            nc.tensor.transpose(turned[:, b, :], zp_row[:, b * P : (b + 1) * P], identity[:])
+        nc.vector.tensor_copy(zp_row[:, tokens(0, 2)], zp_table[:].indirect(entries(0, 2)))
+        nc.scalar.activation(zp_row[:, tokens(2, CHUNKS)], zp_table[:].indirect(entries(2, CHUNKS)), COPY)
+        turned = psum.tile([P, CHUNKS, P], F32, name="turned")
+        for c in range(CHUNKS):
+            nc.tensor.transpose(turned[:, c, :], zp_row[:, tokens(c, c + 1)], identity[:])
+        zp_cols = keep.tile([P, CHUNKS], F32, name="zp_cols")
+        nc.vector.tensor_copy(zp_cols[:], turned[:, :, P - 1])
+        spread = psum.tile([P, CHUNKS, P], F32, name="spread")
+        for c in range(CHUNKS):
+            nc.tensor.transpose(spread[:, c, :], zp_cols[:, c : c + 1].to_broadcast([P, P]), identity[:])
+        csum_turned = psum.tile([P, P], F32, name="csum_turned")
+        nc.tensor.transpose(csum_turned[:], csum_rows[:], identity[:])
+        csum_cols = keep.tile([P, HALVES], F32, name="csum_cols")
+        nc.vector.tensor_copy(csum_cols[:], csum_turned[:, P - HALVES :])
 
-        def pair_views(z, u):
-            pairs = keep.tile([P, 2 * T], BF16, name=f"pairs{z}{u}")
-            return pairs, pairs[:].rearrange("p (t e) -> p t e", e=2), raw[z, u][:].rearrange("p (e t) -> p t e", e=2)
+        def words(z, lo, hi):
+            return grouped[z, lo][:]
 
-        def cast_whole(u):
-            pairs, target, source = pair_views(0, u)
-            nc.scalar.copy(target[:, :SCALAR_SHARE, :], source[:, :SCALAR_SHARE, :])
-            nc.vector.tensor_copy(target[:, SCALAR_SHARE:, :], source[:, SCALAR_SHARE:, :])
-            return pairs[:].bitcast(U32)
+        def gather_stepped(z, t):
+            nc.vector.tensor_copy(words(z, 0, 1)[:, :, t], rows[z, t][:].indirect(entries(0, 1)))
 
-        def quantise(grouped, width, name):
-            codes = keep.tile([P, width], U32, name=f"codes{name}", align_bytes=64)
-            scales = keep.tile([P, width], U8, name=f"scales{name}", align_bytes=64)
-            nc.vector.quantize_mx(out=codes[:].bitcast(FP8X4), scales=scales[:], in_=grouped)
-            return codes, scales
+        def gather_late(z, t, c):
+            nc.scalar.activation(late[z, c][:, t - 2, :], rows[z, t][:].indirect(entries(c, c + 1)), COPY)
 
-        def multiply(acc, z, h, codes, scales):
-            channels = slice(h * P, (h + 1) * P)
-            nc.tensor.matmul_mx(
-                out=acc[:],
-                lhsT=w_codes[z][:, channels].bitcast(FP8X4),
-                lhsT_scale=w_scales[:, z, channels],
-                rhs=codes.bitcast(FP8X4),
-                rhs_scale=scales,
-                start=(z == 0),
-                stop=(z == PASSES - 1),
+        def merge_late(z, c):
+            nc.vector.tensor_copy(words(z, c, c + 1)[:, :, 2:], late[z, c][:].rearrange("p t n -> p n t"))
+
+        quantised = {}
+
+        def quantise(z, lo, hi):
+            width = (hi - lo) * CHUNK
+            codes = keep.tile([P, width], U32, name=f"codes{z}{lo}", align_bytes=64)
+            scales = keep.tile([P, width], U8, name=f"scales{z}{lo}", align_bytes=64)
+            nc.vector.quantize_mx(
+                out=codes[:].bitcast(FP8X4), scales=scales[:], in_=words(z, lo, hi).rearrange("p n t -> p (n t)")
             )
+            for c in range(lo, hi):
+                quantised[z, c] = codes[:, tokens(c - lo, c - lo + 1)], scales[:, tokens(c - lo, c - lo + 1)]
 
-        def entries(c, width):
-            return offsets[:, c * width // 16 : (c + 1) * width // 16]
+        accs = [psum.tile([P, HALVES, CHUNK], F32, name=f"acc{c}") for c in range(CHUNKS)]
 
-        def woven(grouped, dtype):
-            return grouped.bitcast(dtype).rearrange("p (n u) -> p n u", u=2)
-
-        picked0 = keep.tile([P, 2, 2, WIDE], U32, name="picked0")
-        nc.vector.tensor_copy(picked0[:, :, 0, :], cast_whole(0).indirect(offsets[:]))
-        window = cast_whole(1)
-        zp_cols = raw[0, 1][:, :BLOCKS]
-        nc.scalar.copy(zp_cols, turned[:, :, P - 1])
-        spread = psum.tile([P, BLOCKS, P], F32, name="spread", tag="bank7")
-        for b in range(BLOCKS):
-            nc.tensor.transpose(spread[:, b, :], zp_cols[:, b : b + 1].to_broadcast([P, P]), identity[:])
-        for c in range(2):
-            nc.vector.tensor_copy(picked0[:, c, 1, :], window.indirect(entries(c, WIDE)))
-        grouped0 = [keep.tile([P, 4 * WIDE], BF16, name=f"grouped0_{c}", align_bytes=64) for c in range(2)]
-        for c in range(2):
-            nc.vector.tensor_copy(woven(grouped0[c][:], F32), picked0[:, c].bitcast(F32).rearrange("p u n -> p n u"))
-        quantised0 = [quantise(grouped0[c][:], WIDE, f"0_{c}") for c in range(2)]
-
-        pairs10, target, source = pair_views(1, 0)
-        for lo, hi in ((0, CUTS[0]), (CUTS[0], T)):
-            nc.scalar.copy(target[:, lo:hi, :], source[:, lo:hi, :])
-        picked1 = keep.tile([P, CHUNKS, 2, CHUNK], U32, name="picked1")
-        nc.vector.tensor_copy(picked1[:, :, 0, :], pairs10[:].bitcast(U32).indirect(offsets[:]))
-
-        pairs11, target, source = pair_views(1, 1)
-        for lo, hi in ((0, CUTS[1]), (CUTS[1], T)):
-            mid = hi - GPSIMD_SHARE
-            nc.scalar.copy(target[:, lo:mid, :], source[:, lo:mid, :])
-            nc.gpsimd.tensor_scalar(target[:, mid:hi, :], source[:, mid:hi, :], 1.0, 0.0, MULT, ADD)
-        window = pairs11[:].bitcast(U32)
-
-        zp_picked = [raw[1, 1][:, CUTS[1] : CUTS[1] + WIDE]]
-        nc.scalar.copy(zp_picked[0], spread[:, : BLOCKS // 2, :].rearrange("p b n -> p (b n)"))
-        grouped1 = []
-        for c in range(CHUNKS):
-            nc.vector.tensor_copy(picked1[:, c, 1, :], window.indirect(entries(c, CHUNK)))
-            grouped1.append(keep.tile([P, 4 * CHUNK], BF16, name=f"grouped1_{c}", align_bytes=64))
-            nc.scalar.copy(woven(grouped1[c][:], U32), picked1[:, c].rearrange("p u n -> p n u"))
-        zp_late = keep.tile([P, WIDE], F32, name="zp_late", tag="pairs11")
-        zp_picked.append(zp_late[:])
-        nc.scalar.copy(zp_picked[1], spread[:, BLOCKS // 2 :, :].rearrange("p b n -> p (b n)"))
-
-        accs = {}
-        for c in range(CHUNKS):
-            codes, scales = quantised0[c * CHUNK // WIDE]
-            cols = slice(c * CHUNK % WIDE, c * CHUNK % WIDE + CHUNK)
+        def multiply(z, c):
+            codes, scales = quantised[z, c]
             for h in range(HALVES):
-                accs[c, h] = psum.tile([P, CHUNK], F32, name="acc", tag=f"bank{HALVES * c + h}")
-                multiply(accs[c, h], 0, h, codes[:, cols], scales[:, cols])
-        for c in range(CHUNKS):
-            codes, scales = quantise(grouped1[c][:], CHUNK, f"1_{c}")
-            for h in range(HALVES):
-                multiply(accs[c, h], 1, h, codes[:], scales[:])
+                channels = slice(h * P, (h + 1) * P)
+                nc.tensor.matmul_mx(
+                    out=accs[c][:, h, :],
+                    lhsT=w_codes[z][:, channels].bitcast(FP8X4),
+                    lhsT_scale=w_scales[:, z, channels],
+                    rhs=codes.bitcast(FP8X4),
+                    rhs_scale=scales,
+                    start=(z == 0 and h == 0),
+                    stop=(z == PASSES - 1 and h == HALVES - 1),
+                )
 
-        differences = keep.tile([P, CHUNKS, HALVES, CHUNK], F32, name="differences", tag="picked1")
+        for t in range(2):
+            nc.vector.tensor_copy(early0[:, t, tokens(0, 1)], rows[0, t][:].indirect(entries(0, 1)))
+            nc.scalar.activation(early0[:, t, tokens(1, CHUNKS)], rows[0, t][:].indirect(entries(1, CHUNKS)), COPY)
+        for c in range(CHUNKS):
+            nc.vector.tensor_copy(grouped[0, c][:, :, :2], early0[:, :, tokens(c, c + 1)].rearrange("p t n -> p n t"))
+        gather_stepped(0, 2)
+        for c in range(1, CHUNKS):
+            gather_late(0, 2, c)
+        gather_stepped(0, 3)
+        for c in range(1, CHUNKS):
+            gather_late(0, 3, c)
+            merge_late(0, c)
+            quantise(0, c - 1, c)
+            multiply(0, c - 1)
+        gather_stepped(1, 0)
+        quantise(0, CHUNKS - 1, CHUNKS)
+        multiply(0, CHUNKS - 1)
+
+        gather_stepped(1, 1)
+        for t in range(2):
+            nc.scalar.activation(early1[:, t, :], rows[1, t][:].indirect(entries(1, CHUNKS)), COPY)
+        for c in range(1, CHUNKS):
+            nc.vector.tensor_copy(grouped[1, c][:, :, :2], early1[:, :, tokens(c - 1, c)].rearrange("p t n -> p n t"))
+        gather_stepped(1, 2)
+        for c in range(1, CHUNKS):
+            gather_late(1, 2, c)
+        gather_stepped(1, 3)
+        for c in range(1, CHUNKS):
+            gather_late(1, 3, c)
+            merge_late(1, c)
+            quantise(1, c - 1, c)
+            multiply(1, c - 1)
+        quantise(1, CHUNKS - 1, CHUNKS)
+        multiply(1, CHUNKS - 1)
+
+        zp_picked = rows[1, PACK - 1][:, :S].rearrange("p (c n) -> p c n", n=CHUNK)
+        for lo in range(0, CHUNKS, 2):
+            nc.scalar.copy(zp_picked[:, lo : lo + 2, :], spread[:, lo : lo + 2, :])
+
         out_view = out.rearrange("(h p) j -> p h j", p=P)
         for c in range(CHUNKS):
-            cols = slice(c * CHUNK, (c + 1) * CHUNK)
-            zp_chunk = zp_picked[c * CHUNK // WIDE][:, c * CHUNK % WIDE : c * CHUNK % WIDE + CHUNK]
+            cols = tokens(c, c + 1)
+            negated = keep.tile([P, HALVES, CHUNK], F32, name=f"negated{c}")
             result = keep.tile([P, HALVES, CHUNK], F32, name=f"result{c}")
-            by_halves = c in (0, CHUNKS - 1)
             for h in range(HALVES):
-                negated = differences[:, c, h, :]
-                nc.vector.scalar_tensor_tensor(negated, zp_chunk, csum_cols[:, h : h + 1], accs[c, h][:], MULT, SUBTRACT)
-                nc.scalar.activation(result[:, h, :], negated, GELU, bias=zero_bias[:], scale=-1.0)
-                if by_halves:
-                    nc.sync.dma_start(out_view[:, h, cols], result[:, h, :])
-            if not by_halves:
-                nc.sync.dma_start(out_view[:, :, cols], result[:])
+                nc.vector.scalar_tensor_tensor(
+                    negated[:, h, :], zp_picked[:, c, :], csum_cols[:, h : h + 1], accs[c][:, h, :], MULT, SUBTRACT
+                )
+            parts = [slice(0, HALVES)] if c < CHUNKS - 1 else [slice(h, h + 1) for h in range(HALVES)]
+            for part in parts:
+                nc.scalar.activation(result[:, part, :], negated[:, part, :], GELU, bias=zero_bias[:], scale=-1.0)
+                nc.sync.dma_start(out_view[:, part, cols], result[:, part, :])

@@ -66,9 +66,16 @@ def tile_picked_zeropt_gelu_l_kernel(tc, xT, zp, csum, w1_words, w1_scales, offs
         for t in range(PACK):
             load_row(nc.sync, 1, t)
 
-        w_codes = [keep.tile([P, N], U32, name=f"w_codes{z}", align_bytes=64) for z in range(PASSES)]
-        for z in range(PASSES):
-            nc.sync.dma_start(w_codes[z][:].bitcast(I32), w1_words[z].rearrange("p n t -> p (n t)").bitcast(I32))
+        w_codes = {}
+        for h in range(HALVES):
+            first = keep.tile([P, P], U32, name=f"w_first{h}", align_bytes=64)
+            source = w1_words[0].rearrange("p n t -> p (n t)")[:, h * P * PACK : (h + 1) * P * PACK]
+            nc.sync.dma_start(first[:].bitcast(I32), source.bitcast(I32))
+            w_codes[0, h] = first[:]
+        second = keep.tile([P, N], U32, name="w_second", align_bytes=64)
+        nc.sync.dma_start(second[:].bitcast(I32), w1_words[1].rearrange("p n t -> p (n t)").bitcast(I32))
+        for h in range(HALVES):
+            w_codes[1, h] = second[:, h * P : (h + 1) * P]
 
         zero_in = keep.tile([P, 1], F32, name="zero_in")
         zero_bias = keep.tile([P, 1], F32, name="zero_bias")
@@ -97,7 +104,7 @@ def tile_picked_zeropt_gelu_l_kernel(tc, xT, zp, csum, w1_words, w1_scales, offs
         zp_row = keep.tile([P, S], F32, name="zp_row")
         nc.vector.tensor_copy(zp_row[:, tokens(0, 2)], zp_table[:].indirect(entries(0, 2)))
         nc.scalar.activation(zp_row[:, tokens(2, CHUNKS)], zp_table[:].indirect(entries(2, CHUNKS)), COPY)
-        turned = psum.tile([P, CHUNKS, P], F32, name="turned")
+        turned = psum.tile([P, CHUNKS, P], F32, name="turned", tag="bank20")
         for c in range(CHUNKS):
             nc.tensor.transpose(turned[:, c, :], zp_row[:, tokens(c, c + 1)], identity[:])
         zp_cols = keep.tile([P, CHUNKS], F32, name="zp_cols")
@@ -105,7 +112,7 @@ def tile_picked_zeropt_gelu_l_kernel(tc, xT, zp, csum, w1_words, w1_scales, offs
         spread = psum.tile([P, CHUNKS, P], F32, name="spread")
         for c in range(CHUNKS):
             nc.tensor.transpose(spread[:, c, :], zp_cols[:, c : c + 1].to_broadcast([P, P]), identity[:])
-        csum_turned = psum.tile([P, P], F32, name="csum_turned")
+        csum_turned = psum.tile([P, P], F32, name="csum_turned", tag="bank30")
         nc.tensor.transpose(csum_turned[:], csum_rows[:], identity[:])
         csum_cols = keep.tile([P, HALVES], F32, name="csum_cols")
         nc.vector.tensor_copy(csum_cols[:], csum_turned[:, P - HALVES :])
@@ -134,20 +141,25 @@ def tile_picked_zeropt_gelu_l_kernel(tc, xT, zp, csum, w1_words, w1_scales, offs
             for c in range(lo, hi):
                 quantised[z, c] = codes[:, tokens(c - lo, c - lo + 1)], scales[:, tokens(c - lo, c - lo + 1)]
 
-        accs = [psum.tile([P, HALVES, CHUNK], F32, name=f"acc{c}") for c in range(CHUNKS)]
+        shared = psum.tile([P, 2, CHUNK], F32, name="shared")
+        accs = {(c, 1): shared[:, c, :] for c in range(2)}
+        for c in range(CHUNKS):
+            for h in range(HALVES):
+                if (c, h) not in accs:
+                    accs[c, h] = psum.tile([P, CHUNK], F32, name="acc", tag=f"bank{c}{h}")[:]
 
         def multiply(z, c):
             codes, scales = quantised[z, c]
             for h in range(HALVES):
                 channels = slice(h * P, (h + 1) * P)
                 nc.tensor.matmul_mx(
-                    out=accs[c][:, h, :],
-                    lhsT=w_codes[z][:, channels].bitcast(FP8X4),
+                    out=accs[c, h],
+                    lhsT=w_codes[z, h].bitcast(FP8X4),
                     lhsT_scale=w_scales[:, z, channels],
                     rhs=codes.bitcast(FP8X4),
                     rhs_scale=scales,
-                    start=(z == 0 and h == 0),
-                    stop=(z == PASSES - 1 and h == HALVES - 1),
+                    start=(z == 0 and (c, h) != (1, 1)),
+                    stop=(z == PASSES - 1 and (c, h) != (0, 1)),
                 )
 
         for t in range(2):
@@ -190,15 +202,13 @@ def tile_picked_zeropt_gelu_l_kernel(tc, xT, zp, csum, w1_words, w1_scales, offs
             nc.scalar.copy(zp_picked[:, lo : lo + 2, :], spread[:, lo : lo + 2, :])
 
         out_view = out.rearrange("(h p) j -> p h j", p=P)
-        for c in range(CHUNKS):
-            cols = tokens(c, c + 1)
-            negated = keep.tile([P, HALVES, CHUNK], F32, name=f"negated{c}")
-            result = keep.tile([P, HALVES, CHUNK], F32, name=f"result{c}")
+        for lo in range(0, CHUNKS, 2):
             for h in range(HALVES):
-                nc.vector.scalar_tensor_tensor(
-                    negated[:, h, :], zp_picked[:, c, :], csum_cols[:, h : h + 1], accs[c][:, h, :], MULT, SUBTRACT
-                )
-            parts = [slice(0, HALVES)] if c < CHUNKS - 1 else [slice(h, h + 1) for h in range(HALVES)]
-            for part in parts:
-                nc.scalar.activation(result[:, part, :], negated[:, part, :], GELU, bias=zero_bias[:], scale=-1.0)
-                nc.sync.dma_start(out_view[:, part, cols], result[:, part, :])
+                result = keep.tile([P, 2, CHUNK], F32, name=f"result{lo}{h}")
+                for c in (lo, lo + 1):
+                    negated = keep.tile([P, CHUNK], F32, name=f"negated{c}{h}")
+                    nc.vector.scalar_tensor_tensor(
+                        negated[:], zp_picked[:, c, :], csum_cols[:, h : h + 1], accs[c, h], MULT, SUBTRACT
+                    )
+                    nc.scalar.activation(result[:, c - lo, :], negated[:], GELU, bias=zero_bias[:], scale=-1.0)
+                nc.sync.dma_start(out_view[:, h, tokens(lo, lo + 2)], result[:].rearrange("p c n -> p (c n)"))

@@ -39,19 +39,27 @@ def tile_picked_zeropt_gelu_l_kernel(tc, xT, zp, csum, w1_words, w1_scales, offs
         csum_rows = keep.tile([P, P], F32, name="csum_rows")
 
         rows = {}
+        pair = keep.tile([P, 2 * T], F32, name="pair", align_bytes=64)
         for z in range(PASSES):
             for t in range(PACK):
-                rows[z, t] = keep.tile([P, T], F32, name=f"row{z}{t}", align_bytes=64)
+                if z == 0 and t < 2:
+                    rows[z, t] = pair[:, t * T : (t + 1) * T]
+                else:
+                    rows[z, t] = keep.tile([P, T], F32, name=f"row{z}{t}", align_bytes=64)[:]
 
-        def load_row(queue, z, t, parts=slice(0, P)):
+        def load_pair(queue, parts):
+            source = xT[:K_PASS, :].rearrange("(p u e) n -> p u (e n)", u=2, e=2)
+            queue.dma_start(pair[parts, :], source[parts, 0, :])
+
+        def load_row(queue, z, t):
             source = xT[z * K_PASS : (z + 1) * K_PASS, :].rearrange("(p t) n -> p t n", t=PACK)
-            queue.dma_start(rows[z, t][parts, :], source[parts, t, :])
+            queue.dma_start(rows[z, t], source[:, t, :])
 
-        load_row(nc.scalar, 0, 0, slice(0, P, 2))
+        load_pair(nc.scalar, slice(0, P, 2))
         nc.sync.dma_start(zp_table[P - 1 :, :], zp[0:1, :])
         nc.sync.dma_start(csum_rows[P - HALVES :, :], csum.rearrange("(h p) o -> h (p o)", p=P))
-        load_row(nc.sync, 0, 0, slice(1, P, 2))
-        for t in range(1, PACK):
+        load_pair(nc.sync, slice(1, P, 2))
+        for t in range(2, PACK):
             load_row(nc.sync, 0, t)
 
         w_scales = keep.tile([P, PASSES, N], U8, name="w_scales", align_bytes=64)
@@ -92,12 +100,14 @@ def tile_picked_zeropt_gelu_l_kernel(tc, xT, zp, csum, w1_words, w1_scales, offs
         for z in range(PASSES):
             for c in range(CHUNKS):
                 grouped[z, c] = keep.tile([P, CHUNK, PACK], BF16, name=f"grouped{z}{c}", align_bytes=64)
-        early0 = keep.tile([P, 2, S], BF16, name="early0")
+        early0 = keep.tile([P, 2, S], F32, name="early0")
         early1 = keep.tile([P, 2, S - CHUNK], BF16, name="early1")
+        late1 = keep.tile([P, 2, S - CHUNK], BF16, name="late1")
         late = {}
-        for z in range(PASSES):
-            for c in range(1, CHUNKS):
-                late[z, c] = keep.tile([P, 2, CHUNK], BF16, name=f"late{z}{c}")
+        late0 = keep.tile([P, 2, S - CHUNK], BF16, name="late0")
+        for c in range(1, CHUNKS):
+            late[0, c] = late0[:, :, (c - 1) * CHUNK : c * CHUNK]
+            late[1, c] = late1[:, :, (c - 1) * CHUNK : c * CHUNK]
 
         identity = keep.tile([P, P], F32, name="identity")
         make_identity(nc, identity[:])
@@ -121,13 +131,13 @@ def tile_picked_zeropt_gelu_l_kernel(tc, xT, zp, csum, w1_words, w1_scales, offs
             return grouped[z, lo][:]
 
         def gather_stepped(z, t):
-            nc.vector.tensor_copy(words(z, 0, 1)[:, :, t], rows[z, t][:].indirect(entries(0, 1)))
+            nc.vector.tensor_copy(words(z, 0, 1)[:, :, t], rows[z, t].indirect(entries(0, 1)))
 
         def gather_late(z, t, c):
-            nc.scalar.activation(late[z, c][:, t - 2, :], rows[z, t][:].indirect(entries(c, c + 1)), COPY)
+            nc.scalar.activation(late[z, c][:, t - 2, :], rows[z, t].indirect(entries(c, c + 1)), COPY)
 
         def merge_late(z, c):
-            nc.vector.tensor_copy(words(z, c, c + 1)[:, :, 2:], late[z, c][:].rearrange("p t n -> p n t"))
+            nc.vector.tensor_copy(words(z, c, c + 1)[:, :, 2:], late[z, c].rearrange("p t n -> p n t"))
 
         quantised = {}
 
@@ -163,13 +173,12 @@ def tile_picked_zeropt_gelu_l_kernel(tc, xT, zp, csum, w1_words, w1_scales, offs
                 )
 
         for t in range(2):
-            nc.vector.tensor_copy(early0[:, t, tokens(0, 1)], rows[0, t][:].indirect(entries(0, 1)))
-            nc.scalar.activation(early0[:, t, tokens(1, CHUNKS)], rows[0, t][:].indirect(entries(1, CHUNKS)), COPY)
+            nc.vector.tensor_copy(early0[:, t, tokens(0, 2)], rows[0, t].indirect(entries(0, 2)))
+            nc.scalar.activation(early0[:, t, tokens(2, CHUNKS)], rows[0, t].indirect(entries(2, CHUNKS)), COPY)
         for c in range(CHUNKS):
             nc.vector.tensor_copy(grouped[0, c][:, :, :2], early0[:, :, tokens(c, c + 1)].rearrange("p t n -> p n t"))
         gather_stepped(0, 2)
-        for c in range(1, CHUNKS):
-            gather_late(0, 2, c)
+        nc.scalar.activation(late0[:, 0, :], rows[0, 2].indirect(entries(1, CHUNKS)), COPY)
         gather_stepped(0, 3)
         for c in range(1, CHUNKS):
             gather_late(0, 3, c)
@@ -182,12 +191,11 @@ def tile_picked_zeropt_gelu_l_kernel(tc, xT, zp, csum, w1_words, w1_scales, offs
 
         gather_stepped(1, 1)
         for t in range(2):
-            nc.scalar.activation(early1[:, t, :], rows[1, t][:].indirect(entries(1, CHUNKS)), COPY)
+            nc.scalar.activation(early1[:, t, :], rows[1, t].indirect(entries(1, CHUNKS)), COPY)
         for c in range(1, CHUNKS):
             nc.vector.tensor_copy(grouped[1, c][:, :, :2], early1[:, :, tokens(c - 1, c)].rearrange("p t n -> p n t"))
         gather_stepped(1, 2)
-        for c in range(1, CHUNKS):
-            gather_late(1, 2, c)
+        nc.scalar.activation(late1[:, 0, :], rows[1, 2].indirect(entries(1, CHUNKS)), COPY)
         gather_stepped(1, 3)
         for c in range(1, CHUNKS):
             gather_late(1, 3, c)

@@ -152,15 +152,15 @@ def tile_picked_zeropt_gelu_l_kernel(tc, xT, zp, csum, w1_words, w1_scales, offs
                 quantised[z, c] = codes[:, tokens(c - lo, c - lo + 1)], scales[:, tokens(c - lo, c - lo + 1)]
 
         shared = psum.tile([P, 2, CHUNK], F32, name="shared")
-        accs = {(c, 1): shared[:, c, :] for c in range(2)}
+        accs = {(c, 1): shared[:, c - 2, :] for c in range(2, CHUNKS)}
         for c in range(CHUNKS):
             for h in range(HALVES):
                 if (c, h) not in accs:
                     accs[c, h] = psum.tile([P, CHUNK], F32, name="acc", tag=f"bank{c}{h}")[:]
 
-        def multiply(z, c):
+        def multiply(z, c, halves=range(HALVES)):
             codes, scales = quantised[z, c]
-            for h in range(HALVES):
+            for h in halves:
                 channels = slice(h * P, (h + 1) * P)
                 nc.tensor.matmul_mx(
                     out=accs[c, h],
@@ -168,8 +168,8 @@ def tile_picked_zeropt_gelu_l_kernel(tc, xT, zp, csum, w1_words, w1_scales, offs
                     lhsT_scale=w_scales[:, z, channels],
                     rhs=codes.bitcast(FP8X4),
                     rhs_scale=scales,
-                    start=(z == 0 and (c, h) != (1, 1)),
-                    stop=(z == PASSES - 1 and (c, h) != (0, 1)),
+                    start=(z == 0 and (c, h) != (3, 1)),
+                    stop=(z == PASSES - 1 and (c, h) != (2, 1)),
                 )
 
         for t in range(2):
@@ -201,9 +201,12 @@ def tile_picked_zeropt_gelu_l_kernel(tc, xT, zp, csum, w1_words, w1_scales, offs
             gather_late(1, 3, c)
             merge_late(1, c)
             quantise(1, c - 1, c)
-            multiply(1, c - 1)
         quantise(1, CHUNKS - 1, CHUNKS)
-        multiply(1, CHUNKS - 1)
+        for h in range(HALVES):
+            for c in range(2):
+                multiply(1, c, [h])
+        for c in range(2, CHUNKS):
+            multiply(1, c)
 
         zp_picked = rows[1, PACK - 1][:, :S].rearrange("p (c n) -> p c n", n=CHUNK)
         for lo in range(0, CHUNKS, 2):
@@ -219,4 +222,7 @@ def tile_picked_zeropt_gelu_l_kernel(tc, xT, zp, csum, w1_words, w1_scales, offs
                         negated[:], zp_picked[:, c, :], csum_cols[:, h : h + 1], accs[c, h], MULT, SUBTRACT
                     )
                     nc.scalar.activation(result[:, c - lo, :], negated[:], GELU, bias=zero_bias[:], scale=-1.0)
-                nc.sync.dma_start(out_view[:, h, tokens(lo, lo + 2)], result[:].rearrange("p c n -> p (c n)"))
+                    if (lo, h) == (0, 0):
+                        nc.sync.dma_start(out_view[:, h, tokens(c, c + 1)], result[:, c, :])
+                if (lo, h) != (0, 0):
+                    nc.sync.dma_start(out_view[:, h, tokens(lo, lo + 2)], result[:].rearrange("p c n -> p (c n)"))

@@ -38,29 +38,23 @@ def tile_picked_zeropt_gelu_l_kernel(tc, xT, zp, csum, w1_words, w1_scales, offs
         zp_table = keep.tile([P, T], F32, name="zp_table")
         csum_rows = keep.tile([P, P], F32, name="csum_rows")
 
-        rows = {}
         pair = keep.tile([P, 2 * T], F32, name="pair", align_bytes=64)
+        pair_source = xT[:K_PASS, :].rearrange("(p u e) n -> p u (e n)", u=2, e=2)[:, 0, :]
+        rows = {}
         for z in range(PASSES):
-            for t in range(PACK):
-                if z == 0 and t < 2:
-                    rows[z, t] = pair[:, t * T : (t + 1) * T]
-                else:
-                    rows[z, t] = keep.tile([P, T], F32, name=f"row{z}{t}", align_bytes=64)[:]
+            for t in range(2 if z == 0 else 0, PACK):
+                rows[z, t] = keep.tile([P, T], F32, name=f"row{z}{t}", align_bytes=64)
 
-        def load_pair(queue, parts):
-            source = xT[:K_PASS, :].rearrange("(p u e) n -> p u (e n)", u=2, e=2)
-            queue.dma_start(pair[parts, :], source[parts, 0, :])
-
-        def load_row(queue, z, t):
+        def load_row(z, t):
             source = xT[z * K_PASS : (z + 1) * K_PASS, :].rearrange("(p t) n -> p t n", t=PACK)
-            queue.dma_start(rows[z, t], source[:, t, :])
+            nc.sync.dma_start(rows[z, t][:], source[:, t, :])
 
-        load_pair(nc.scalar, slice(0, P, 2))
+        nc.scalar.dma_start(pair[0:P:2, :], pair_source[0:P:2, :])
         nc.sync.dma_start(zp_table[P - 1 :, :], zp[0:1, :])
         nc.sync.dma_start(csum_rows[P - HALVES :, :], csum.rearrange("(h p) o -> h (p o)", p=P))
-        load_pair(nc.sync, slice(1, P, 2))
+        nc.sync.dma_start(pair[1:P:2, :], pair_source[1:P:2, :])
         for t in range(2, PACK):
-            load_row(nc.sync, 0, t)
+            load_row(0, t)
 
         w_scales = keep.tile([P, PASSES, N], U8, name="w_scales", align_bytes=64)
         nc.vector.memset(w_scales[:].rearrange("p z n -> p (z n)").bitcast(I32), 0)
@@ -72,7 +66,7 @@ def tile_picked_zeropt_gelu_l_kernel(tc, xT, zp, csum, w1_words, w1_scales, offs
         nc.vector.memset(zp_table[: P - 1, :], 0.0)
         nc.vector.memset(csum_rows[: P - HALVES, :], 0.0)
         for t in range(PACK):
-            load_row(nc.sync, 1, t)
+            load_row(1, t)
 
         w_codes = {}
         for h in range(HALVES):
@@ -96,19 +90,6 @@ def tile_picked_zeropt_gelu_l_kernel(tc, xT, zp, csum, w1_words, w1_scales, offs
         def tokens(lo, hi):
             return slice(lo * CHUNK, hi * CHUNK)
 
-        grouped = {}
-        for z in range(PASSES):
-            for c in range(CHUNKS):
-                grouped[z, c] = keep.tile([P, CHUNK, PACK], BF16, name=f"grouped{z}{c}", align_bytes=64)
-        early0 = keep.tile([P, 2, S], F32, name="early0")
-        early1 = keep.tile([P, 2, S - CHUNK], BF16, name="early1")
-        late1 = keep.tile([P, 2, S - CHUNK], BF16, name="late1")
-        late = {}
-        late0 = keep.tile([P, 2, S - CHUNK], BF16, name="late0")
-        for c in range(1, CHUNKS):
-            late[0, c] = late0[:, :, (c - 1) * CHUNK : c * CHUNK]
-            late[1, c] = late1[:, :, (c - 1) * CHUNK : c * CHUNK]
-
         identity = keep.tile([P, P], F32, name="identity")
         make_identity(nc, identity[:])
         zp_row = keep.tile([P, S], F32, name="zp_row")
@@ -127,102 +108,112 @@ def tile_picked_zeropt_gelu_l_kernel(tc, xT, zp, csum, w1_words, w1_scales, offs
         csum_cols = keep.tile([P, HALVES], F32, name="csum_cols")
         nc.vector.tensor_copy(csum_cols[:], csum_turned[:, P - HALVES :])
 
-        def words(z, lo, hi):
-            return grouped[z, lo][:]
-
-        def gather_stepped(z, t):
-            nc.vector.tensor_copy(words(z, 0, 1)[:, :, t], rows[z, t].indirect(entries(0, 1)))
-
-        def gather_late(z, t, c):
-            nc.scalar.activation(late[z, c][:, t - 2, :], rows[z, t].indirect(entries(c, c + 1)), COPY)
-
-        def merge_late(z, c):
-            nc.vector.tensor_copy(words(z, c, c + 1)[:, :, 2:], late[z, c].rearrange("p t n -> p n t"))
+        grouped = {}
+        for z in range(PASSES):
+            for c in range(CHUNKS):
+                grouped[z, c] = keep.tile([P, CHUNK, PACK], BF16, name=f"grouped{z}{c}", align_bytes=64)
 
         quantised = {}
 
-        def quantise(z, lo, hi):
-            width = (hi - lo) * CHUNK
-            codes = keep.tile([P, width], U32, name=f"codes{z}{lo}", align_bytes=64)
-            scales = keep.tile([P, width], U8, name=f"scales{z}{lo}", align_bytes=64)
+        def quantise(z, c):
+            codes = keep.tile([P, CHUNK], U32, name=f"codes{z}{c}", align_bytes=64)
+            scales = keep.tile([P, CHUNK], U8, name=f"scales{z}{c}", align_bytes=64)
             nc.vector.quantize_mx(
-                out=codes[:].bitcast(FP8X4), scales=scales[:], in_=words(z, lo, hi).rearrange("p n t -> p (n t)")
+                out=codes[:].bitcast(FP8X4), scales=scales[:], in_=grouped[z, c][:].rearrange("p n t -> p (n t)")
             )
-            for c in range(lo, hi):
-                quantised[z, c] = codes[:, tokens(c - lo, c - lo + 1)], scales[:, tokens(c - lo, c - lo + 1)]
+            quantised[z, c] = codes[:], scales[:]
 
-        shared = psum.tile([P, 2, CHUNK], F32, name="shared")
-        accs = {(c, 1): shared[:, c - 2, :] for c in range(2, CHUNKS)}
+        shared = psum.tile([P, HALVES, CHUNK], F32, name="shared", tag="bank30")
+        accs = {(CHUNKS - 1, h): shared[:, h, :] for h in range(HALVES)}
+        for c in range(CHUNKS - 1):
+            for h in range(HALVES):
+                accs[c, h] = psum.tile([P, CHUNK], F32, name="acc", tag=f"bank{c}{h}")[:]
+
+        def multiply(z, c, h):
+            codes, scales = quantised[z, c]
+            nc.tensor.matmul_mx(
+                out=accs[c, h],
+                lhsT=w_codes[z, h].bitcast(FP8X4),
+                lhsT_scale=w_scales[:, z, h * P : (h + 1) * P],
+                rhs=codes.bitcast(FP8X4),
+                rhs_scale=scales,
+                start=(z == 0 and (c, h) != (CHUNKS - 1, 1)),
+                stop=(z == PASSES - 1 and (c, h) != (CHUNKS - 1, 0)),
+            )
+
+        planes = [keep.tile([P, PACK, S], BF16, name=f"planes{z}", align_bytes=64) for z in range(PASSES)]
+
+        def gather(engine, z, t, lo, hi):
+            window = rows[z, t][:].indirect(entries(lo, hi))
+            if engine is nc.scalar:
+                nc.scalar.activation(planes[z][:, t, tokens(lo, hi)], window, COPY)
+            else:
+                nc.vector.tensor_copy(planes[z][:, t, tokens(lo, hi)], window)
+
+        def merge(engine, z, c, lo, hi):
+            source = planes[z][:, lo:hi, tokens(c, c + 1)].rearrange("p t n -> p n t")
+            if engine is nc.scalar:
+                nc.scalar.copy(grouped[z, c][:, :, lo:hi], source)
+            else:
+                nc.vector.tensor_copy(grouped[z, c][:, :, lo:hi], source)
+
+        runs = []
+        for half in range(2):
+            run = keep.tile([P, 5, CHUNK], BF16, name=f"run{half}", align_bytes=64)
+            picked = entries(2 * half, 2 * half + 2)
+            nc.scalar.activation(run[:, :2, :].rearrange("p c n -> p (c n)"), pair[:].indirect(picked), COPY)
+            nc.vector.tensor_copy(run[:, 2::2, :], pair[:, T:].indirect(picked))
+            runs.append(run)
+        for c in range(CHUNKS):
+            both = runs[c // 2][:, 0:3:2, :] if c % 2 == 0 else runs[c // 2][:, 1:5:3, :]
+            nc.vector.tensor_copy(grouped[0, c][:, :, :2], both.rearrange("p t n -> p n t"))
+        gather(nc.scalar, 0, 2, 0, CHUNKS)
+        gather(nc.vector, 0, 3, 0, 2)
+        gather(nc.scalar, 0, 3, 2, CHUNKS)
+        for c in range(CHUNKS):
+            merge(nc.vector, 0, c, 2, PACK)
+        for c in range(CHUNKS):
+            quantise(0, c)
+        for h in range(HALVES):
+            for c in range(CHUNKS):
+                multiply(0, c, h)
+
+        gather(nc.scalar, 1, 0, 0, CHUNKS)
+        gather(nc.scalar, 1, 1, 2, CHUNKS)
+        gather(nc.vector, 1, 1, 0, 2)
+        for c in (2, 3):
+            merge(nc.vector, 1, c, 0, 2)
+        gather(nc.scalar, 1, 2, 1, 2)
+        gather(nc.vector, 1, 2, 0, 1)
+        gather(nc.scalar, 1, 2, 2, CHUNKS)
+        for c in (1, 0):
+            merge(nc.vector, 1, c, 0, 3)
+
+        for c in range(2):
+            nc.vector.tensor_copy(grouped[1, c][:, :, 3], rows[1, 3][:].indirect(entries(c, c + 1)))
+        gather(nc.scalar, 1, 3, 2, 3)
+        gather(nc.scalar, 1, 3, 3, 4)
+        merge(nc.scalar, 1, 2, 2, PACK)
+        quantise(1, 0)
+        merge(nc.vector, 1, 3, 2, PACK)
+        for c in range(1, CHUNKS):
+            quantise(1, c)
         for c in range(CHUNKS):
             for h in range(HALVES):
-                if (c, h) not in accs:
-                    accs[c, h] = psum.tile([P, CHUNK], F32, name="acc", tag=f"bank{c}{h}")[:]
-
-        def multiply(z, c, halves=range(HALVES)):
-            codes, scales = quantised[z, c]
-            for h in halves:
-                channels = slice(h * P, (h + 1) * P)
-                nc.tensor.matmul_mx(
-                    out=accs[c, h],
-                    lhsT=w_codes[z, h].bitcast(FP8X4),
-                    lhsT_scale=w_scales[:, z, channels],
-                    rhs=codes.bitcast(FP8X4),
-                    rhs_scale=scales,
-                    start=(z == 0 and (c, h) != (3, 1)),
-                    stop=(z == PASSES - 1 and (c, h) != (2, 1)),
-                )
-
-        for t in range(2):
-            nc.vector.tensor_copy(early0[:, t, tokens(0, 2)], rows[0, t].indirect(entries(0, 2)))
-            nc.scalar.activation(early0[:, t, tokens(2, CHUNKS)], rows[0, t].indirect(entries(2, CHUNKS)), COPY)
-        for c in range(CHUNKS):
-            nc.vector.tensor_copy(grouped[0, c][:, :, :2], early0[:, :, tokens(c, c + 1)].rearrange("p t n -> p n t"))
-        gather_stepped(0, 2)
-        nc.scalar.activation(late0[:, 0, :], rows[0, 2].indirect(entries(1, CHUNKS)), COPY)
-        gather_stepped(0, 3)
-        for c in range(1, CHUNKS):
-            gather_late(0, 3, c)
-            merge_late(0, c)
-            quantise(0, c - 1, c)
-            multiply(0, c - 1)
-        gather_stepped(1, 0)
-        quantise(0, CHUNKS - 1, CHUNKS)
-        multiply(0, CHUNKS - 1)
-
-        gather_stepped(1, 1)
-        for t in range(2):
-            nc.scalar.activation(early1[:, t, :], rows[1, t].indirect(entries(1, CHUNKS)), COPY)
-        for c in range(1, CHUNKS):
-            nc.vector.tensor_copy(grouped[1, c][:, :, :2], early1[:, :, tokens(c - 1, c)].rearrange("p t n -> p n t"))
-        gather_stepped(1, 2)
-        nc.scalar.activation(late1[:, 0, :], rows[1, 2].indirect(entries(1, CHUNKS)), COPY)
-        gather_stepped(1, 3)
-        for c in range(1, CHUNKS):
-            gather_late(1, 3, c)
-            merge_late(1, c)
-            quantise(1, c - 1, c)
-        quantise(1, CHUNKS - 1, CHUNKS)
-        for h in range(HALVES):
-            for c in range(2):
-                multiply(1, c, [h])
-        for c in range(2, CHUNKS):
-            multiply(1, c)
+                multiply(1, c, h)
 
         zp_picked = rows[1, PACK - 1][:, :S].rearrange("p (c n) -> p c n", n=CHUNK)
         for lo in range(0, CHUNKS, 2):
             nc.scalar.copy(zp_picked[:, lo : lo + 2, :], spread[:, lo : lo + 2, :])
 
         out_view = out.rearrange("(h p) j -> p h j", p=P)
-        for lo in range(0, CHUNKS, 2):
+        for lo, hi in ((0, 1), (1, 3), (3, 4)):
             for h in range(HALVES):
-                result = keep.tile([P, 2, CHUNK], F32, name=f"result{lo}{h}")
-                for c in (lo, lo + 1):
+                result = keep.tile([P, hi - lo, CHUNK], F32, name=f"result{lo}{h}")
+                for c in range(lo, hi):
                     negated = keep.tile([P, CHUNK], F32, name=f"negated{c}{h}")
                     nc.vector.scalar_tensor_tensor(
                         negated[:], zp_picked[:, c, :], csum_cols[:, h : h + 1], accs[c, h], MULT, SUBTRACT
                     )
                     nc.scalar.activation(result[:, c - lo, :], negated[:], GELU, bias=zero_bias[:], scale=-1.0)
-                    if (lo, h) == (0, 0):
-                        nc.sync.dma_start(out_view[:, h, tokens(c, c + 1)], result[:, c, :])
-                if (lo, h) != (0, 0):
-                    nc.sync.dma_start(out_view[:, h, tokens(lo, lo + 2)], result[:].rearrange("p c n -> p (c n)"))
+                nc.sync.dma_start(out_view[:, h, tokens(lo, hi)], result[:].rearrange("p c n -> p (c n)"))

@@ -25,6 +25,7 @@ PASSES = K // K_PASS
 HALVES = N // P
 CHUNK = 128
 CHUNKS = S // CHUNK
+LAST = (CHUNKS - 1, HALVES - 1)
 
 
 def tile_picked_zeropt_gelu_l_kernel(tc, xT, zp, csum, w1_words, w1_scales, offs, out):
@@ -123,22 +124,21 @@ def tile_picked_zeropt_gelu_l_kernel(tc, xT, zp, csum, w1_words, w1_scales, offs
             )
             quantised[z, c] = codes[:], scales[:]
 
-        shared = psum.tile([P, HALVES, CHUNK], F32, name="shared", tag="bank30")
-        accs = {(CHUNKS - 1, h): shared[:, h, :] for h in range(HALVES)}
-        for c in range(CHUNKS - 1):
-            for h in range(HALVES):
-                accs[c, h] = psum.tile([P, CHUNK], F32, name="acc", tag=f"bank{c}{h}")[:]
+        accs = {}
 
         def multiply(z, c, h):
             codes, scales = quantised[z, c]
+            if z == 0:
+                bank = "bank00" if (c, h) == LAST else f"bank{c}{h}"
+                accs[c, h] = psum.tile([P, CHUNK], F32, name="acc", tag=bank)[:]
             nc.tensor.matmul_mx(
                 out=accs[c, h],
                 lhsT=w_codes[z, h].bitcast(FP8X4),
                 lhsT_scale=w_scales[:, z, h * P : (h + 1) * P],
                 rhs=codes.bitcast(FP8X4),
                 rhs_scale=scales,
-                start=(z == 0 and (c, h) != (CHUNKS - 1, 1)),
-                stop=(z == PASSES - 1 and (c, h) != (CHUNKS - 1, 0)),
+                start=(z == 0),
+                stop=(z == PASSES - 1),
             )
 
         planes = [keep.tile([P, PACK, S], BF16, name=f"planes{z}", align_bytes=64) for z in range(PASSES)]
@@ -150,12 +150,15 @@ def tile_picked_zeropt_gelu_l_kernel(tc, xT, zp, csum, w1_words, w1_scales, offs
             else:
                 nc.vector.tensor_copy(planes[z][:, t, tokens(lo, hi)], window)
 
-        def merge(engine, z, c, lo, hi):
-            source = planes[z][:, lo:hi, tokens(c, c + 1)].rearrange("p t n -> p n t")
+        def merge(engine, z, c, lo, hi, part=slice(0, CHUNK)):
+            source = planes[z][:, lo:hi, tokens(c, c + 1)][:, :, part].rearrange("p t n -> p n t")
             if engine is nc.scalar:
-                nc.scalar.copy(grouped[z, c][:, :, lo:hi], source)
+                nc.scalar.copy(grouped[z, c][:, part, lo:hi], source)
             else:
-                nc.vector.tensor_copy(grouped[z, c][:, :, lo:hi], source)
+                nc.vector.tensor_copy(grouped[z, c][:, part, lo:hi], source)
+
+        def gather_stepped(t, c):
+            nc.vector.tensor_copy(grouped[1, c][:, :, t], rows[1, t][:].indirect(entries(c, c + 1)))
 
         runs = []
         for half in range(2):
@@ -176,44 +179,55 @@ def tile_picked_zeropt_gelu_l_kernel(tc, xT, zp, csum, w1_words, w1_scales, offs
             quantise(0, c)
         for h in range(HALVES):
             for c in range(CHUNKS):
-                multiply(0, c, h)
+                if (c, h) != LAST:
+                    multiply(0, c, h)
 
         gather(nc.scalar, 1, 0, 0, CHUNKS)
         gather(nc.scalar, 1, 1, 2, CHUNKS)
         gather(nc.vector, 1, 1, 0, 2)
-        for c in (2, 3):
+        for c in (2, 3, 0):
             merge(nc.vector, 1, c, 0, 2)
         gather(nc.scalar, 1, 2, 1, 2)
-        gather(nc.vector, 1, 2, 0, 1)
+        gather_stepped(2, 0)
         gather(nc.scalar, 1, 2, 2, CHUNKS)
-        for c in (1, 0):
-            merge(nc.vector, 1, c, 0, 3)
+        merge(nc.vector, 1, 1, 0, 3)
 
         for c in range(2):
-            nc.vector.tensor_copy(grouped[1, c][:, :, 3], rows[1, 3][:].indirect(entries(c, c + 1)))
+            gather_stepped(3, c)
         gather(nc.scalar, 1, 3, 2, 3)
         gather(nc.scalar, 1, 3, 3, 4)
         merge(nc.scalar, 1, 2, 2, PACK)
-        quantise(1, 0)
-        merge(nc.vector, 1, 3, 2, PACK)
-        for c in range(1, CHUNKS):
+        merge(nc.scalar, 1, 3, 2, PACK, slice(0, CHUNK // 2))
+        for c in range(2):
             quantise(1, c)
-        for c in range(CHUNKS):
-            for h in range(HALVES):
-                multiply(1, c, h)
+        merge(nc.vector, 1, 3, 2, PACK, slice(CHUNK // 2, CHUNK))
+        for c in range(2, CHUNKS):
+            quantise(1, c)
 
         zp_picked = rows[1, PACK - 1][:, :S].rearrange("p (c n) -> p c n", n=CHUNK)
         for lo in range(0, CHUNKS, 2):
             nc.scalar.copy(zp_picked[:, lo : lo + 2, :], spread[:, lo : lo + 2, :])
 
-        out_view = out.rearrange("(h p) j -> p h j", p=P)
-        for lo, hi in ((0, 1), (1, 3), (3, 4)):
+        for lo in range(0, CHUNKS, 2):
             for h in range(HALVES):
-                result = keep.tile([P, hi - lo, CHUNK], F32, name=f"result{lo}{h}")
-                for c in range(lo, hi):
+                for c in (lo, lo + 1):
+                    if (c, h) != LAST:
+                        multiply(1, c, h)
+
+        out_view = out.rearrange("(h p) j -> p h j", p=P)
+        for lo in range(0, CHUNKS, 2):
+            for h in range(HALVES):
+                result = keep.tile([P, 2, CHUNK], F32, name=f"result{lo}{h}")
+                for c in (lo, lo + 1):
+                    if (c, h) == LAST:
+                        for z in range(PASSES):
+                            multiply(z, c, h)
                     negated = keep.tile([P, CHUNK], F32, name=f"negated{c}{h}")
                     nc.vector.scalar_tensor_tensor(
                         negated[:], zp_picked[:, c, :], csum_cols[:, h : h + 1], accs[c, h], MULT, SUBTRACT
                     )
                     nc.scalar.activation(result[:, c - lo, :], negated[:], GELU, bias=zero_bias[:], scale=-1.0)
-                nc.sync.dma_start(out_view[:, h, tokens(lo, hi)], result[:].rearrange("p c n -> p (c n)"))
+                    if (lo, h) == (0, 0):
+                        nc.sync.dma_start(out_view[:, h, tokens(c, c + 1)], result[:, c, :])
+                if (lo, h) != (0, 0):
+                    nc.sync.dma_start(out_view[:, h, tokens(lo, lo + 2)], result[:].rearrange("p c n -> p (c n)"))

@@ -183,9 +183,10 @@ def tile_picked_zeropt_gelu_l_kernel(tc, xT, zp, csum, w1_words, w1_scales, offs
                     multiply(0, c, h)
 
         gather(nc.scalar, 1, 0, 0, CHUNKS)
-        gather(nc.scalar, 1, 1, 2, CHUNKS)
-        gather(nc.vector, 1, 1, 0, 2)
-        for c in (2, 3, 0):
+        gather(nc.vector, 1, 1, 0, 1)
+        for c in (2, 3, 1):
+            gather(nc.scalar, 1, 1, c, c + 1)
+        for c in (0, 2, 3):
             merge(nc.vector, 1, c, 0, 2)
         gather(nc.scalar, 1, 2, 1, 2)
         gather_stepped(2, 0)

from contextlib import ExitStack

import concourse.mybir as mybir
from concourse.masks import make_identity

K, T, S, N = 1024, 1024, 512, 256
FLOPS = 2 * K * S * N

F32 = mybir.dt.float32
BF16 = mybir.dt.bfloat16
I32 = mybir.dt.int32
U32 = mybir.dt.uint32
U16 = mybir.dt.uint16
U8 = mybir.dt.uint8
FP8X4 = mybir.dt.float8_e4m3fn_x4
GELU = mybir.ActivationFunctionType.Gelu_apprx_tanh
COPY = mybir.ActivationFunctionType.Copy
MULT = mybir.AluOpType.mult
SUBTRACT = mybir.AluOpType.subtract

P = 128
PACK = 4
K_PASS = P * PACK
PASSES = K // K_PASS
HALVES = N // P
CHUNK = 128
CHUNKS = S // CHUNK
LAST = (CHUNKS - 1, HALVES - 1)


def tile_picked_zeropt_gelu_l_kernel(tc, xT, zp, csum, w1_words, w1_scales, offs, out):
    nc = tc.nc
    with ExitStack() as ctx:
        keep = ctx.enter_context(tc.tile_pool(name="keep", bufs=1))
        psum = ctx.enter_context(tc.psum_pool(name="psum", bufs=1))

        offsets = keep.tile([P, S // 16], U16, name="offsets")
        nc.sync.dma_start(offsets[:], offs)
        zp_table = keep.tile([P, T], F32, name="zp_table")
        csum_rows = keep.tile([P, P], F32, name="csum_rows")

        pair = keep.tile([P, 2 * T], F32, name="pair", align_bytes=64)
        pair_source = xT[:K_PASS, :].rearrange("(p u e) n -> p u (e n)", u=2, e=2)[:, 0, :]
        rows = {}
        for z in range(PASSES):
            for t in range(2 if z == 0 else 0, PACK):
                rows[z, t] = keep.tile([P, T], F32, name=f"row{z}{t}", align_bytes=64)

        def load_row(z, t):
            source = xT[z * K_PASS : (z + 1) * K_PASS, :].rearrange("(p t) n -> p t n", t=PACK)
            nc.sync.dma_start(rows[z, t][:], source[:, t, :])

        nc.scalar.dma_start(pair[0:P:2, :], pair_source[0:P:2, :])
        nc.sync.dma_start(zp_table[P - 1 :, :], zp[0:1, :])
        nc.sync.dma_start(csum_rows[P - HALVES :, :], csum.rearrange("(h p) o -> h (p o)", p=P))
        nc.sync.dma_start(pair[1:P:2, :], pair_source[1:P:2, :])
        for t in range(2, PACK):
            load_row(0, t)

        w_scales = keep.tile([P, PASSES, N], U8, name="w_scales", align_bytes=64)
        nc.vector.memset(w_scales[:].rearrange("p z n -> p (z n)").bitcast(I32), 0)
        for q in range(4):
            nc.sync.dma_start(
                w_scales[32 * q : 32 * q + 4, :, :].bitcast(I32),
                w1_scales[:, 4 * q : 4 * q + 4, :].rearrange("z r n -> r z n").bitcast(I32),
            )
        nc.vector.memset(zp_table[: P - 1, :], 0.0)
        nc.vector.memset(csum_rows[: P - HALVES, :], 0.0)
        for t in range(PACK):
            load_row(1, t)

        w_codes = {}
        for h in range(HALVES):
            first = keep.tile([P, P], U32, name=f"w_first{h}", align_bytes=64)
            source = w1_words[0].rearrange("p n t -> p (n t)")[:, h * P * PACK : (h + 1) * P * PACK]
            nc.sync.dma_start(first[:].bitcast(I32), source.bitcast(I32))
            w_codes[0, h] = first[:]
        second = keep.tile([P, N], U32, name="w_second", align_bytes=64)
        nc.sync.dma_start(second[:].bitcast(I32), w1_words[1].rearrange("p n t -> p (n t)").bitcast(I32))
        for h in range(HALVES):
            w_codes[1, h] = second[:, h * P : (h + 1) * P]

        zero_in = keep.tile([P, 1], F32, name="zero_in")
        zero_bias = keep.tile([P, 1], F32, name="zero_bias")
        nc.vector.memset(zero_in[:], 0.0)
        nc.scalar.activation(zero_bias[:], zero_in[:], GELU)

        def entries(lo, hi):
            return offsets[:, lo * CHUNK // 16 : hi * CHUNK // 16]

        def tokens(lo, hi):
            return slice(lo * CHUNK, hi * CHUNK)

        identity = keep.tile([P, P], F32, name="identity")
        make_identity(nc, identity[:])
        zp_row = keep.tile([P, S], F32, name="zp_row")
        nc.vector.tensor_copy(zp_row[:, tokens(0, 2)], zp_table[:].indirect(entries(0, 2)))
        nc.scalar.activation(zp_row[:, tokens(2, CHUNKS)], zp_table[:].indirect(entries(2, CHUNKS)), COPY)
        turned = psum.tile([P, CHUNKS, P], F32, name="turned", tag="bank20")
        for c in range(CHUNKS):
            nc.tensor.transpose(turned[:, c, :], zp_row[:, tokens(c, c + 1)], identity[:])
        zp_cols = keep.tile([P, CHUNKS], F32, name="zp_cols")
        nc.vector.tensor_copy(zp_cols[:], turned[:, :, P - 1])
        spread = psum.tile([P, CHUNKS, P], F32, name="spread")
        for c in range(CHUNKS):
            nc.tensor.transpose(spread[:, c, :], zp_cols[:, c : c + 1].to_broadcast([P, P]), identity[:])
        csum_turned = psum.tile([P, P], F32, name="csum_turned", tag="bank30")
        nc.tensor.transpose(csum_turned[:], csum_rows[:], identity[:])
        csum_cols = keep.tile([P, HALVES], F32, name="csum_cols")
        nc.vector.tensor_copy(csum_cols[:], csum_turned[:, P - HALVES :])

        grouped = {}
        for z in range(PASSES):
            for c in range(CHUNKS):
                grouped[z, c] = keep.tile([P, CHUNK, PACK], BF16, name=f"grouped{z}{c}", align_bytes=64)

        quantised = {}

        def quantise(z, c):
            codes = keep.tile([P, CHUNK], U32, name=f"codes{z}{c}", align_bytes=64)
            scales = keep.tile([P, CHUNK], U8, name=f"scales{z}{c}", align_bytes=64)
            nc.vector.quantize_mx(
                out=codes[:].bitcast(FP8X4), scales=scales[:], in_=grouped[z, c][:].rearrange("p n t -> p (n t)")
            )
            quantised[z, c] = codes[:], scales[:]

        accs = {}

        def multiply(z, c, h):
            codes, scales = quantised[z, c]
            if z == 0:
                bank = "bank00" if (c, h) == LAST else f"bank{c}{h}"
                accs[c, h] = psum.tile([P, CHUNK], F32, name="acc", tag=bank)[:]
            nc.tensor.matmul_mx(
                out=accs[c, h],
                lhsT=w_codes[z, h].bitcast(FP8X4),
                lhsT_scale=w_scales[:, z, h * P : (h + 1) * P],
                rhs=codes.bitcast(FP8X4),
                rhs_scale=scales,
                start=(z == 0),
                stop=(z == PASSES - 1),
            )

        planes = [keep.tile([P, PACK, S], BF16, name=f"planes{z}", align_bytes=64) for z in range(PASSES)]

        def gather(engine, z, t, lo, hi):
            window = rows[z, t][:].indirect(entries(lo, hi))
            if engine is nc.scalar:
                nc.scalar.activation(planes[z][:, t, tokens(lo, hi)], window, COPY)
            else:
                nc.vector.tensor_copy(planes[z][:, t, tokens(lo, hi)], window)

        def merge(engine, z, c, lo, hi, part=slice(0, CHUNK)):
            source = planes[z][:, lo:hi, tokens(c, c + 1)][:, :, part].rearrange("p t n -> p n t")
            if engine is nc.scalar:
                nc.scalar.copy(grouped[z, c][:, part, lo:hi], source)
            else:
                nc.vector.tensor_copy(grouped[z, c][:, part, lo:hi], source)

        def gather_stepped(t, c):
            nc.vector.tensor_copy(grouped[1, c][:, :, t], rows[1, t][:].indirect(entries(c, c + 1)))

        runs = []
        for half in range(2):
            run = keep.tile([P, 5, CHUNK], BF16, name=f"run{half}", align_bytes=64)
            picked = entries(2 * half, 2 * half + 2)
            nc.scalar.activation(run[:, :2, :].rearrange("p c n -> p (c n)"), pair[:].indirect(picked), COPY)
            nc.vector.tensor_copy(run[:, 2::2, :], pair[:, T:].indirect(picked))
            runs.append(run)
        for c in range(CHUNKS):
            both = runs[c // 2][:, 0:3:2, :] if c % 2 == 0 else runs[c // 2][:, 1:5:3, :]
            nc.vector.tensor_copy(grouped[0, c][:, :, :2], both.rearrange("p t n -> p n t"))
        gather(nc.scalar, 0, 2, 0, CHUNKS)
        gather(nc.vector, 0, 3, 0, 2)
        gather(nc.scalar, 0, 3, 2, CHUNKS)
        for c in range(CHUNKS):
            merge(nc.vector, 0, c, 2, PACK)
        for c in range(CHUNKS):
            quantise(0, c)
        for h in range(HALVES):
            for c in range(CHUNKS):
                if (c, h) != LAST:
                    multiply(0, c, h)

        gather(nc.scalar, 1, 0, 0, CHUNKS)
        gather(nc.vector, 1, 1, 0, 1)
        for c in (2, 3, 1):
            gather(nc.scalar, 1, 1, c, c + 1)
        for c in (0, 2, 3):
            merge(nc.vector, 1, c, 0, 2)
        gather(nc.scalar, 1, 2, 1, 2)
        gather_stepped(2, 0)
        gather(nc.scalar, 1, 2, 2, CHUNKS)
        merge(nc.vector, 1, 1, 0, 3)

        for c in range(2):
            gather_stepped(3, c)
        gather(nc.scalar, 1, 3, 2, 3)
        gather(nc.scalar, 1, 3, 3, 4)
        merge(nc.scalar, 1, 2, 2, PACK)
        merge(nc.scalar, 1, 3, 2, PACK, slice(0, CHUNK // 2))
        for c in range(2):
            quantise(1, c)
        merge(nc.vector, 1, 3, 2, PACK, slice(CHUNK // 2, CHUNK))
        for c in range(2, CHUNKS):
            quantise(1, c)

        zp_picked = rows[1, PACK - 1][:, :S].rearrange("p (c n) -> p c n", n=CHUNK)
        for lo in range(0, CHUNKS, 2):
            nc.scalar.copy(zp_picked[:, lo : lo + 2, :], spread[:, lo : lo + 2, :])

        for lo in range(0, CHUNKS, 2):
            for h in range(HALVES):
                for c in (lo, lo + 1):
                    if (c, h) != LAST:
                        multiply(1, c, h)

        out_view = out.rearrange("(h p) j -> p h j", p=P)
        for lo in range(0, CHUNKS, 2):
            for h in range(HALVES):
                result = keep.tile([P, 2, CHUNK], F32, name=f"result{lo}{h}")
                for c in (lo, lo + 1):
                    if (c, h) == LAST:
                        for z in range(PASSES):
                            multiply(z, c, h)
                    negated = keep.tile([P, CHUNK], F32, name=f"negated{c}{h}")
                    nc.vector.scalar_tensor_tensor(
                        negated[:], zp_picked[:, c, :], csum_cols[:, h : h + 1], accs[c, h], MULT, SUBTRACT
                    )
                    nc.scalar.activation(result[:, c - lo, :], negated[:], GELU, bias=zero_bias[:], scale=-1.0)
                    if (lo, h) == (0, 0):
                        nc.sync.dma_start(out_view[:, h, tokens(c, c + 1)], result[:, c, :])
                if (lo, h) != (0, 0):
                    nc.sync.dma_start(out_view[:, h, tokens(lo, lo + 2)], result[:].rearrange("p c n -> p (c n)"))
